import numpy as np, ml_dtypes
CORES = [24,25,26,27,28,29,30,31]
N = 8
import mx_ref
BF = ml_dtypes.bfloat16
def entries(a):
    return np.ascontiguousarray(a.T).reshape(-1)
def table(e):
    return np.ascontiguousarray(np.reshape(e, (-1, 16)).T).astype(np.int32)
def cols(t, e):
    v = np.concatenate([t.reshape(128, -1, 4), np.zeros((128, 1, 4), BF)], axis=1)
    return np.ascontiguousarray(v[:, e]).reshape(128, -1)
def cut(t, i, w=512):
    return t[:, w * i:w * i + w]
def f(rng, *shape):
    return mx_ref.flush((rng.standard_normal(shape, dtype=np.float32) * np.exp2(rng.integers(-2, 3, shape[:-1] + (1,)))).astype(BF))
def wide(rng, *shape, cols=0):
    v = rng.standard_normal(shape, dtype=np.float32) * np.exp2(rng.integers(-12, 13, shape)).astype(np.float32)
    if cols: v *= np.repeat(np.exp2(rng.integers(-cols, cols + 1, shape[:-2] + (1, shape[-1] // 4))) * (rng.random(shape[:-2] + (1, shape[-1] // 4)) > 0.0625), 4, axis=-1).astype(np.float32)
    return mx_ref.flush(v.astype(BF))
TB, T, CAPP, O = 512, 512, 48, 1
def lists(rng, case=""):
    o = []; odd = rng.permutation(N)
    for r in range(N):
        lo, hi = {"one": (1, 1), "full": (CAPP, CAPP), "runs": (1, CAPP // 2), "none": (1, CAPP)}.get(case, (0, CAPP))
        n = rng.integers(lo, hi + 1, N)
        if case == "none":
            if r == odd[0]: n[:] = 0; n[rng.integers(0, N)] = 1
            elif r == odd[1]: n[r] = 0
            elif r == odd[2]: n[np.arange(N) != r] = 0
            else: n[rng.permutation(N)[:rng.integers(1, N)]] = 0
        if n.sum() == 0: n[rng.integers(0, N)] = 1
        if case == "full": named = [np.append([0, TB - 1], 1 + rng.permutation(TB - 2)[:n[q] - 2]) for q in range(N)]
        else: named = [rng.permutation(TB)[:n[q]] for q in range(N)]
        pool = rng.permutation(np.concatenate([q * TB + named[q] for q in range(N)]))
        i = np.arange(len(pool))
        k = T - len(pool)
        i = np.concatenate([i, (rng.random(k) * rng.random(k) * len(pool)).astype(int)])
        i = np.sort(i) if case == "runs" else rng.permutation(i)
        o.append(table(pool[i]))
    return {"want": np.stack(o)}
def setup_inputs(rng):
    return {"x": f(rng, N, 128, 4 * TB), "w": f(rng, N, 128, 512 * O), **lists(rng)}
def setup_inputs_one(rng):
    return {**setup_inputs(rng), **lists(rng, "one")}
def setup_inputs_full(rng):
    return {**setup_inputs(rng), **lists(rng, "full")}
def setup_inputs_runs(rng):
    return {**setup_inputs(rng), **lists(rng, "runs")}
def setup_inputs_none(rng):
    return {**setup_inputs(rng), **lists(rng, "none")}
def setup_inputs_spread(rng):
    d = setup_inputs(rng); d["x"] = wide(rng, N, 128, 4 * TB, cols=8); return d
def check_inputs(d):
    b = []
    for r in range(N):
        e = entries(d["want"][r])
        if e.min() < 0 or e.max() >= N * TB or any(len(np.unique(e[e // TB == q])) > CAPP for q in range(N)): b.append("want")
    return b
def reference(x, w, want):
    every = np.concatenate([x[q] for q in range(N)], axis=1)
    y = np.zeros((N, 128, O * T), np.float32)
    for r in range(N):
        t = mx_ref.quantize(cols(every, entries(want[r])))
        for o in range(O):
            y[r][:, T * o:T * o + T] = mx_ref.matmul(mx_ref.quantize(np.ascontiguousarray(cut(w[r], o))), t)
    return {"y": y}

@@ -1,0 +1,321 @@
+from concourse.bass import DstId, RemoteDMATransfer
+from concourse.mybir import dt, AluOpType, AxisListType, ActivationFunctionType
+
+A = AluOpType
+F = ActivationFunctionType
+CAP = 48
+PL = 528
+BIG = 8192.0
+
+
+def sb(kind, **widths):
+    return {k: ("sbuf", [128, n], kind) for k, n in widths.items()}
+
+
+SCRATCH = {
+    **sb("int32", Lw=32, D=16, Ei=32, pid=1, p4=1, q0=32, q1=32, q2=32, q3=32),
+    **sb("uint16", off0=32, EO=32, off1=16, O=24, OO=4, OP=64, FO=32),
+    **sb("float32", Cf=4, Cb=4, Dc=16, X=512, R=512, row=128, bt=1, p4f=1, t2=1, gsh=1, did=4, k16=4, thr=4, K=4, G=40, TG=32,
+         J0=512, J1=512, LR=32, X1=32, X3=32, Z=384, yv=256, ys=256, o1=32, q4=32, xa=32, xb=32, xc=32, xd=32, xe=32, xf=32),
+    **sb("bfloat16", E0=512, E1=384, E2=256, E3=128, NB=2048, MK=640, ones=256, Win=8704, OB=512, CW=544, J2=512,
+         x0=2048, XP=4 * PL, wt=512, H=1344, HO=512, Pr=1024, PT=1024),
+    **sb("float8_e4m3fn_x4", Q=256, Q2=128, QO=128, QW=128, CR=336),
+    **sb("uint8", SQ=256, S2=128, SO=128, SW=128, SR=336),
+    "pa": ("psum", [128, 512], "float32"), "pb": ("psum", [128, 512], "float32"), "po": ("psum", [128, 512], "float32"),
+}
+SEMAPHORES = ["v", "s", "g", "t", "ld", "lz", "lw", "lx", "lv", "ly", "la", "a0", "a1", "a2", "out"]
+
+
+def rank_program(g, core, T, topo):
+    r = T.rank_of(core)
+    if r is None:
+        return
+    N = len(T.cores)
+    S = T.sem
+    cnt = {"v": 0, "s": 0, "g": 0, "t": 0}
+    queues = {"v": g.vector, "s": g.scalar, "g": g, "t": g.tensor, "y": g.sync}
+    waited = {}
+
+    def need(qn, *toks):
+        for name, n in toks:
+            if waited.get((qn, name), 0) < n:
+                waited[(qn, name)] = n
+                queues[qn].wait_ge(S[name], n)
+
+    def done(qn, ins):
+        ins.then_inc(S[qn], 1)
+        cnt[qn] += 1
+        return (qn, cnt[qn])
+
+    V, Sc = g.vector, g.scalar
+
+    def iota(ap, n, base=0, cm=0, step=1):
+        return done("g", g.iota(ap, [[step, n]], base, cm, allow_small_or_imprecise_dtypes=True))
+
+    for e in range(4):
+        q = g.sync if e % 2 == 0 else g.scalar
+        q.dma_start(T.D[32 * e:32 * e + 32, :], T.want[:, :]).then_inc(S.ld, 16)
+
+    kEi = done("g", g.iota(T.Ei[:, :], [[1, 16], [0, 2]], 0, 0))
+    kPid = done("g", g.iota(T.pid[:, :], [[1, 1]], 0, 1))
+    kBt = iota(T.bt[:, :], 1, int(BIG), int(BIG))
+    kRow = iota(T.row[:, :], 128)
+    kK16 = iota(T.k16[:, :], 4, 0, 1, 16)
+    kDid = iota(T.did[:, :], 4, 4096, 4)
+    kOnes = iota(T.ones[:, :], 256, 1, step=0)
+    kWin2 = iota(T.Win[:, 6144:6656], 512, step=0)
+    iota(T.CW[:, 0:16], 16, step=0)
+    kCz = iota(T.CW[:, 528:544], 16, step=0)
+    kMz = done("v", V.memset(T.MK[:, 128:640], 0.0))
+    need("v", kEi)
+    kEO = done("v", V.tensor_copy(T.EO[:, :], T.Ei[:, :]))
+    need("v", kPid)
+    kP4 = done("v", V.tensor_scalar(T.p4[:, :], T.pid[:, :], 4, None, A.arith_shift_right))
+    need("v", kP4)
+    kP4f = done("v", V.tensor_copy(T.p4f[:, :], T.p4[:, :]))
+    z3 = done("v", V.memset(T.LR[:, 31:32], 0.0))
+    need("y", kMz)
+    for lo in (4096, 2048):
+        g.sync.dma_start(T.Win[:, lo:lo + 512], T.MK[:, 128:640]).then_inc(S.lz, 16)
+    for h in range(4):
+        g.sync.dma_start(T.Lw[16 * h:16 * h + 16, :], T.want[:, :]).then_inc(S.lw, 16)
+    g.sync.dma_start(T.x0[:, :], T.x[:, :]).then_inc(S.lx, 16)
+    g.sync.dma_start(T.wt[:, :], T.w[:, :]).then_inc(S.lv, 16)
+
+    need("v", ("ld", 64))
+    kDc = done("v", V.tensor_scalar(T.Dc[:, :], T.D[:, :], BIG, None, A.mult))
+    need("v", kEO)
+    kXv = done("v", V.tensor_scalar(T.X[:, 0:320], T.D[:, 0:16].indirect(T.EO[:, 0:20]), BIG, None, A.mult))
+    need("s", kDc, kEO)
+    kXs = done("s", Sc.activation(T.X[:, 320:512], T.Dc[:, 0:16].indirect(T.EO[:, 20:32]), F.Copy))
+    need("s", kBt, kRow)
+    kTri = done("s", Sc.activation(T.MK[:, 0:128], T.row[:, :], F.Relu, bias=T.bt[:, 0:1], scale=-BIG))
+    for e in range(4):
+        h = slice(32 * e, 32 * e + 32)
+        kCb = done("s", Sc.activation(T.Cb[h, :], T.Dc[h, e:16:4], F.Copy))
+    need("v", kXv, kXs)
+    kR1 = done("v", V.transpose(T.R[:, 256:512], T.X[:, 256:512]))
+    kR0 = done("v", V.transpose(T.R[:, 0:256], T.X[:, 0:256]))
+    E = [T.E0, T.E1, T.E2, T.E3]
+    need("s", kR1, kCb)
+    kS, kE = {}, {}
+    for k in (3, 2, 1, 0):
+        lo = max(128 * k, 256)
+        kS[k] = done("s", Sc.activation(E[k][:, lo - 128 * k:512 - 128 * k], T.R[:, lo:512], F.Abs, bias=T.Cb[:, k:k + 1], scale=-1.0))
+    kC = done("s", Sc.activation(T.Cf[:, :], T.Cb[:, :], F.Copy, scale=1.0 / BIG))
+    need("s", kP4f)
+    kGsh = done("s", Sc.activation(T.gsh[:, :], T.p4f[:, :], F.Identity, bias=4096.0, scale=-512.0))
+    kT2 = done("s", Sc.activation(T.t2[:, :], T.p4f[:, :], F.Identity, bias=0.5, scale=-16.0))
+    need("v", kR0, kCb)
+    for k in (1, 0):
+        kE[k] = done("v", V.tensor_scalar(E[k][:, 0:256 - 128 * k], T.R[:, 128 * k:256], T.Cb[:, k:k + 1], BIG, A.not_equal, A.mult))
+    need("v", kTri, kMz)
+    for k in (3, 2, 1, 0):
+        need("v", kS[k])
+        if k < 2:
+            need("v", kE[k])
+        kN = done("v", V.tensor_tensor_scan(T.NB[:, 640 * k:512 * k + 512], E[k][:, :], T.MK[:, 0:512 - 128 * k], BIG, A.min, A.max))
+    need("v", kN, kDid, kC)
+    kK = done("v", V.tensor_tensor(T.K[:, :], T.did[:, :], T.NB[:, 511:2048:512], A.subtract))
+    need("v", kK)
+    e1 = done("v", V.tensor_tensor(T.G[:, 0:4], T.K[:, :], T.Cf[:, :], A.max))
+    e2 = done("v", V.tensor_tensor(T.G[:, 12:16], T.K[:, :], T.Cf[:, :], A.max))
+    need("v", e1)
+    need("s", e1)
+    done("v", V.tensor_copy(T.G[0:64, 4:8], T.G[64:128, 0:4]))
+    a1 = done("v", V.tensor_copy(T.G[0:64, 8:12], T.G[64:128, 0:4]))
+    done("s", Sc.activation(T.G[64:128, 4:8], T.G[0:64, 0:4], F.Copy))
+    b1 = done("s", Sc.activation(T.G[64:128, 8:12], T.G[0:64, 0:4], F.Copy))
+    need("v", a1, b1, e2)
+    need("s", a1, b1, e2)
+    done("v", V.tensor_copy(T.G[0:32, 16:32], T.G[32:64, 0:16]))
+    done("v", V.tensor_copy(T.G[32:64, 16:32], T.G[0:32, 0:16]))
+    a2 = done("v", V.tensor_copy(T.G[:, 32:40], T.G[:, 0:8]))
+    done("s", Sc.activation(T.G[64:96, 16:32], T.G[96:128, 0:16], F.Copy))
+    b2 = done("s", Sc.activation(T.G[96:128, 16:32], T.G[64:96, 0:16], F.Copy))
+    need("s", kT2, kK16)
+    kThr = done("s", Sc.activation(T.thr[:, :], T.k16[:, :], F.Identity, bias=T.t2[:, 0:1]))
+    need("v", a2, b2)
+    kTG = done("v", V.transpose(T.TG[:, :], T.G[:, 8:40]))
+    need("v", kTG, kGsh)
+    done("v", V.tensor_scalar(T.off1[0:64, :], T.TG[0:64, 0:16], T.gsh[0:64, 0:1], None, A.add))
+    kO1 = done("v", V.tensor_scalar(T.off1[64:128, :], T.TG[64:128, 16:32], T.gsh[64:128, 0:1], None, A.add))
+    need("v", kO1, kOnes, kWin2, ("lz", 32))
+    kSc = done("v", V.tensor_copy(T.Win[:, 0:8704].indirect(T.off1[:, 0:16]), T.ones[:, :]))
+    need("v", kSc)
+    need("s", kSc)
+    done("v", V.tensor_copy(T.OB[0:64, :], T.Win[64:128, 2048:2560]))
+    o1 = done("v", V.tensor_copy(T.OB[64:128, 0:160], T.Win[0:64, 6144:6304]))
+    o2 = done("s", Sc.activation(T.OB[64:128, 160:512], T.Win[0:64, 6304:6656], F.Copy))
+    need("v", o1, o2)
+    kCum = done("v", V.tensor_tensor_scan(T.CW[:, 16:528], T.Win[:, 4096:4608], T.OB[:, :], 0.0, A.add, A.add))
+    need("s", kCum, kThr)
+    done("s", Sc.activation(T.J0[:, :], T.CW[:, 16:528], F.Sign, bias=T.thr[:, 0:1], scale=-1.0, accum_out=T.LR[:, 28:29]))
+    c1 = done("s", Sc.activation(T.J1[:, :], T.CW[:, 16:528], F.Sign, bias=T.thr[:, 1:2], scale=-1.0, accum_out=T.LR[:, 29:30]))
+    need("v", kCum, kThr)
+    kJ2 = done("v", V.tensor_scalar(T.J2[:, :], T.CW[:, 16:528], T.thr[:, 2:3], None, A.is_lt))
+    need("v", kJ2)
+    c2 = done("v", V.tensor_reduce(T.LR[:, 30:31], T.J2[:, :], AxisListType.X, A.add))
+    sent = [0]
+
+    def mask(dst, pick):
+        es = topo.engines(core, dst)
+        m = 0
+        for j in pick(len(es)):
+            m |= 1 << es[j]
+            sent[0] += 1
+        return m
+
+    def at(dst):
+        rid, pid, _ = topo.addr(dst)
+        return DstId(rid=rid, pnc=pid)
+
+    def fused(items):
+        tr = []
+        for d, src, out, sem, pick in items:
+            c = T.cores[d]
+            tr.append(RemoteDMATransfer(dst_ids=[at(c)], dma_engine_mask=mask(c, pick), remote_sem=sem, src=src, dst=out))
+        g.remote_dma_fused(tr, local_sem=S.out)
+
+    def every(i, n):
+        return lambda ne: range(i, ne, n)
+
+    need("g", c1, z3, c2)
+    to = [T.cores[(r - 1 - i) % N] for i in range(7)]
+    g.remote_dma_fused([RemoteDMATransfer(dst_ids=[at(c) for c in to], dma_engine_mask=mask(to[0], every(0, 1)), remote_sem=S.la,
+                                          srcs=[T.LR[:, 28:32]], dsts=[T.LR[:, 4 * i:4 * i + 4] for i in range(7)])], local_sem=S.out)
+    nla = 7 * sent[0]
+
+    need("v", ("lw", 64))
+    done("v", V.tensor_copy(T.off0[0:64, :], T.Lw[0:64, :]))
+    kOff0 = done("v", V.tensor_copy(T.off0[64:128, :], T.Lw[0:64, :]))
+    need("v", kOff0)
+    ko1 = done("v", V.tensor_scalar(T.o1[:, :], T.off0[:, :], T.gsh[:, 0:1], 4608.0, A.add, A.min))
+    kq0 = done("v", V.tensor_copy(T.q0[:, :], T.off0[:, :]))
+    need("v", ko1)
+    done("v", V.tensor_scalar(T.OP[:, 0:64:2], T.o1[:, :], 4095.0, -4080.0, A.max, A.add))
+    kOP = done("v", V.tensor_scalar(T.OP[:, 1:64:2], T.o1[:, :], 4095.0, -4080.0, A.max, A.add))
+    need("v", ("lx", 16))
+    for t in (0, 1, 2):
+        done("v", V.tensor_copy(T.XP[:, PL * t:PL * t + 512], T.x0[:, t:2048:4]))
+    kPad = done("v", V.memset(T.XP[:, 512:4 * PL:PL], 0.0))
+    need("s", ("lx", 16))
+    kPlS = done("s", Sc.activation(T.XP[:, PL * 3:PL * 3 + 512], T.x0[:, 3:2048:4], F.Copy))
+    need("s", kOP, kCz, kCum)
+    kPs = done("s", Sc.activation(T.Pr[:, 384:1024], T.CW[:, 0:544].indirect(T.OP[:, 24:64]), F.Copy))
+    need("v", kOP, kCz, kCum)
+    kPv = done("v", V.tensor_copy(T.Pr[:, 0:384], T.CW[:, 0:544].indirect(T.OP[:, 0:24])))
+
+    a, b = divmod(r, 2)
+    ra = slice(32 * a, 32 * a + 32)
+    need("v", ("la", nla), c1, c2)
+    kX1 = done("v", V.transpose(T.X1[ra, :], T.LR[ra, :]))
+    need("v", kX1)
+    kXd = done("v", V.tensor_copy(T.X1[ra, 16 - 16 * b:32 - 16 * b], T.X1[ra, 16 * b:16 * b + 16]))
+    need("v", kXd)
+    need("s", kXd)
+    todo = [slice(32 * d, 32 * d + 32) for d in range(4) if d != a]
+    kcs = done("s", Sc.activation(T.X1[todo[0], :], T.X1[ra, :], F.Copy))
+    for o in todo[1:]:
+        kcv = done("v", V.tensor_copy(T.X1[o, :], T.X1[ra, :]))
+    need("v", kcs, kcv)
+    kX3 = done("v", V.transpose(T.X3[:, :], T.X1[:, :]))
+    need("v", kX3)
+    done("v", V.tensor_scalar(T.O[:, 0:21:3], T.X3[:, 0:28:4], 0.5, 256.0, A.mult, A.add))
+    done("v", V.tensor_scalar(T.O[:, 1:21:3], T.X3[:, 1:28:4], 0.5, 256.0, A.mult, A.add))
+    kO = done("v", V.tensor_copy(T.O[:, 2:21:3], T.X3[:, 2:28:4]))
+
+    def pick(h, o, t, lo, hi):
+        return h[:, 64 * lo + t:64 * hi:4], T.XP[:, PL * t:PL * t + 513].indirect(o[:, lo:hi])
+
+    part = [(0, 8), (8, 16), (16, 21)]
+    need("s", kO, kPlS, kPad)
+    kh = []
+    for lo, hi in part:
+        for t in (2, 3):
+            k = done("s", Sc.activation(*pick(T.H, T.O, t, lo, hi), F.Copy))
+        kh.append(k)
+    need("v", kO, kPlS, kPad)
+    eng = {2: [every(0, 2), every(1, 2)], 3: [every(0, 2), every(1, 4), every(3, 4)]}
+    flip = {2: [every(1, 2), every(0, 2)], 3: [every(1, 2), every(0, 4), every(2, 4)]}
+    kv = {}
+    for n, ids in enumerate(((0, 1), (2, 3, 4), (5, 6))):
+        for m, t in ((n, 0), (n, 1), (n + 1, 0)):
+            if m < 3 and (m, t) not in kv:
+                kv[m, t] = done("v", V.tensor_copy(*pick(T.H, T.O, t, *part[m])))
+        q, p, lo, c0 = (T.Q, T.SQ, 128 * n, 0) if n < 2 else (T.Q2, T.S2, 0, 208)
+        need("v", kv[n, 0], kv[n, 1], kh[n])
+        kq = done("v", V.quantize_mx(q[:, lo:lo + 128], p[:, lo:lo + 128], T.H[:, 4 * (lo + c0):4 * (lo + c0) + 512]))
+        need("g", kq)
+        to = [((r + 1 + i) % N, slice(CAP * i - c0, CAP * i - c0 + CAP), slice(CAP * i, CAP * i + CAP)) for i in ids]
+        sem = S["a%d" % n]
+        fused([(d, q[:, c].bitcast(dt.uint8), T.CR[:, e].bitcast(dt.uint8), sem, m) for (d, c, e), m in zip(to, eng[len(to)])])
+        fused([(d, p[:, c], T.SR[:, e], sem, m) for (d, c, e), m in zip(to, flip[len(to)])])
+    done("v", V.tensor_scalar(T.OO[:, 0:2], T.X3[:, 28:30], 0.5, 256.0, A.mult, A.add))
+    kOO = done("v", V.tensor_copy(T.OO[:, 2:3], T.X3[:, 30:31]))
+    need("s", kOO)
+    for t in range(4):
+        kHo = done("s", Sc.activation(*pick(T.HO, T.OO, t, 0, 3), F.Copy))
+    need("v", ("lv", 16))
+    kW = done("v", V.quantize_mx(T.QW[:, :], T.SW[:, :], T.wt[:, :]))
+
+    need("v", kPs, kPv)
+    kPT = done("v", V.transpose(T.PT[:, :], T.Pr[:, :]))
+    kHz = done("v", V.memset(T.HO[:, 192:512], 0.0))
+    need("v", kq0)
+    kq1 = done("v", V.tensor_scalar(T.q1[:, :], T.q0[:, :], 9, None, A.arith_shift_right))
+    need("v", kPT)
+    kxa = done("v", V.tensor_tensor(T.xa[:, :], T.PT[:, 0:1024:32], T.PT[:, 16:1024:32], A.add))
+    need("v", kxa)
+    need("s", kxa)
+    x1 = done("v", V.tensor_copy(T.xb[0:64, :], T.xa[64:128, :]))
+    x2 = done("s", Sc.activation(T.xb[64:128, :], T.xa[0:64, :], F.Copy))
+    need("v", kq1)
+    kq2 = done("v", V.tensor_scalar(T.q2[:, :], T.q1[:, :], -1.0, float(r + 7), A.mult, A.add))
+    need("v", kHo, kHz)
+    kqo = done("v", V.quantize_mx(T.QO[:, :], T.SO[:, :], T.HO[:, :]))
+    need("v", x1, x2)
+    kxc = done("v", V.tensor_tensor(T.xc[:, :], T.xa[:, :], T.xb[:, :], A.add))
+    need("v", kq2)
+    kq3 = done("v", V.tensor_scalar(T.q3[:, :], T.q2[:, :], 7, None, A.bitwise_and))
+    need("v", kxc)
+    need("s", kxc)
+    done("v", V.tensor_copy(T.xd[0:32, :], T.xc[32:64, :]))
+    x3 = done("v", V.tensor_copy(T.xd[32:64, :], T.xc[0:32, :]))
+    done("s", Sc.activation(T.xd[64:96, :], T.xc[96:128, :], F.Copy))
+    x4 = done("s", Sc.activation(T.xd[96:128, :], T.xc[64:96, :], F.Copy))
+    need("v", kq3)
+    kq4 = done("v", V.tensor_scalar(T.q4[:, :], T.q3[:, :], 48.0, -1.0, A.mult, A.add))
+    need("v", kq4)
+    kxe = done("v", V.tensor_tensor(T.xe[:, :], T.xc[:, :], T.q4[:, :], A.add))
+    need("v", x3, x4, kxe)
+    kxf = done("v", V.tensor_tensor(T.xf[:, :], T.xe[:, :], T.xd[:, :], A.add))
+    need("v", kxf)
+    kFO = done("v", V.tensor_copy(T.FO[:, :], T.xf[:, :]))
+
+    ts = g.tensor
+    need("t", kW, kqo)
+    m0 = done("t", ts.matmul_mx(T.po[:, 0:128], T.QW[:, :], T.SW[:, :], T.QO[:, :], T.SO[:, :], True, True))
+    need("t", ("a0", 32), ("a1", 32))
+    m1 = done("t", ts.matmul_mx(T.pa[:, 0:240], T.QW[:, :], T.SW[:, :], T.CR[:, 0:240], T.SR[:, 0:240], True, True))
+    need("t", ("a2", 32))
+    m2 = done("t", ts.matmul_mx(T.pb[:, 0:128], T.QW[:, :], T.SW[:, :], T.CR[:, 208:336], T.SR[:, 208:336], True, True))
+
+    need("v", m0)
+    zo = done("v", V.tensor_copy(T.Z[:, 336:384], T.po[:, 0:48]))
+    need("s", m1)
+    za = done("s", Sc.activation(T.Z[:, 0:240], T.pa[:, 0:240], F.Copy))
+    need("v", m2)
+    zb = done("v", V.tensor_copy(T.Z[:, 240:336], T.pb[:, 32:128]))
+    need("v", kFO, zo, za, zb)
+    need("s", kFO, zo, za, zb)
+    for lo, hi, qn in ((0, 6, "y"), (6, 16, "s")):
+        ky = done("v", V.tensor_copy(T.yv[:, 16 * lo:16 * hi], T.Z[:, 0:384].indirect(T.FO[:, lo:hi])))
+        need("y", ky)
+        g.sync.dma_start(T.y[:, 16 * lo:16 * hi], T.yv[:, 16 * lo:16 * hi]).then_inc(S.ly, 16)
+        ky = done("s", Sc.activation(T.ys[:, 16 * lo:16 * hi], T.Z[:, 0:384].indirect(T.FO[:, 16 + lo:16 + hi]), F.Copy))
+        need(qn, ky)
+        queues[qn].dma_start(T.y[:, 256 + 16 * lo:256 + 16 * hi], T.ys[:, 16 * lo:16 * hi]).then_inc(S.ly, 16)
+
+    need("g", ("out", sent[0]), ("v", cnt["v"]), ("s", cnt["s"]), ("g", cnt["g"]), ("t", cnt["t"]))
+    need("g", ("ld", 64), ("lz", 32), ("lw", 64), ("lx", 16), ("lv", 16), ("ly", 64), ("la", nla), ("a0", 32), ("a1", 32), ("a2", 32))

@@ -6,6 +6,10 @@ F = ActivationFunctionType
 CAP = 48
 PL = 528
 BIG = 8192.0
+UP = 1024.0
+WA, WB = 2560, 4608
+CS = 288
+SE = 768
 
 
 def sb(kind, **widths):
@@ -13,17 +17,17 @@ def sb(kind, **widths):
 
 
 SCRATCH = {
-    **sb("int32", Lw=32, D=16, Ei=32, pid=1, p4=1, q0=32, q1=32, q2=32, q3=32),
-    **sb("uint16", off0=32, EO=32, off1=16, O=24, OO=4, OP=64, FO=32),
-    **sb("float32", Cf=4, Cb=4, Dc=16, X=512, R=512, row=128, bt=1, p4f=1, t2=1, gsh=1, did=4, k16=4, thr=4, K=4, G=40, TG=32,
-         J0=512, J1=512, LR=32, X1=32, X3=32, Z=384, yv=256, ys=256, o1=32, q4=32, xa=32, xb=32, xc=32, xd=32, xe=32, xf=32),
-    **sb("bfloat16", E0=512, E1=384, E2=256, E3=128, NB=2048, MK=640, ones=256, Win=8704, OB=512, CW=544, J2=512,
+    **sb("int32", Lw=32, D=8, Ei=8, pid=4, pm=4, p4=1, p43=1, q0=32, q1=32, q2=32, q3=32),
+    **sb("uint16", off0=32, EO=8, off1=16, O=24, OO=4, OP=64, FO=32),
+    **sb("float32", Cf=8, X=128, R=128, row=64, sgn=1, gsh=1, gp=1, k16=4, n=4, am=4, idn=4, thr=4, K=8, K2=8, P1=1, SRC=SE + 4,
+         J0=512, J1=CS, LR=32, X1=32, X3=32, Z=384, yv=256, ys=256, o1=32, q4=32, xa=32, xb=32, xc=32, xd=32, xe=32, xf=32),
+    **sb("bfloat16", E=512, NB=512, MK=256, ones=512, zero=64, Win=6656, M=512, CW=544, J2=512, J3=512 - CS,
          x0=2048, XP=4 * PL, wt=512, H=1344, HO=512, Pr=1024, PT=1024),
     **sb("float8_e4m3fn_x4", Q=256, Q2=128, QO=128, QW=128, CR=336),
     **sb("uint8", SQ=256, S2=128, SO=128, SW=128, SR=336),
     "pa": ("psum", [128, 512], "float32"), "pb": ("psum", [128, 512], "float32"), "po": ("psum", [128, 512], "float32"),
 }
-SEMAPHORES = ["v", "s", "g", "t", "ld", "lz", "lw", "lx", "lv", "ly", "la", "a0", "a1", "a2", "out"]
+SEMAPHORES = ["v", "s", "g", "t", "ld", "lw", "lx", "lv", "ly", "la", "a0", "a1", "a2", "out"]
 
 
 def rank_program(g, core, T, topo):
@@ -48,114 +52,106 @@ def rank_program(g, core, T, topo):
         return (qn, cnt[qn])
 
     V, Sc = g.vector, g.scalar
+    lower, upper = slice(0, 64), slice(64, 128)
+    quad = [slice(32 * e, 32 * e + 32) for e in range(4)]
 
     def iota(ap, n, base=0, cm=0, step=1):
         return done("g", g.iota(ap, [[step, n]], base, cm, allow_small_or_imprecise_dtypes=True))
 
-    for e in range(4):
-        q = g.sync if e % 2 == 0 else g.scalar
-        q.dma_start(T.D[32 * e:32 * e + 32, :], T.want[:, :]).then_inc(S.ld, 16)
-
-    kEi = done("g", g.iota(T.Ei[:, :], [[1, 16], [0, 2]], 0, 0))
-    kPid = done("g", g.iota(T.pid[:, :], [[1, 1]], 0, 1))
-    kBt = iota(T.bt[:, :], 1, int(BIG), int(BIG))
-    kRow = iota(T.row[:, :], 128)
-    kK16 = iota(T.k16[:, :], 4, 0, 1, 16)
-    kDid = iota(T.did[:, :], 4, 4096, 4)
-    kOnes = iota(T.ones[:, :], 256, 1, step=0)
-    kWin2 = iota(T.Win[:, 6144:6656], 512, step=0)
-    iota(T.CW[:, 0:16], 16, step=0)
-    kCz = iota(T.CW[:, 528:544], 16, step=0)
-    kMz = done("v", V.memset(T.MK[:, 128:640], 0.0))
-    need("v", kEi)
-    kEO = done("v", V.tensor_copy(T.EO[:, :], T.Ei[:, :]))
-    need("v", kPid)
-    kP4 = done("v", V.tensor_scalar(T.p4[:, :], T.pid[:, :], 4, None, A.arith_shift_right))
-    need("v", kP4)
-    kP4f = done("v", V.tensor_copy(T.p4f[:, :], T.p4[:, :]))
-    z3 = done("v", V.memset(T.LR[:, 31:32], 0.0))
-    need("y", kMz)
-    for lo in (4096, 2048):
-        g.sync.dma_start(T.Win[:, lo:lo + 512], T.MK[:, 128:640]).then_inc(S.lz, 16)
+    g.sync.dma_start(T.D[:, 0:4], T.want[:, :]).then_inc(S.ld, 16)
+    g.scalar.dma_start(T.D[0:112, 4:8], T.want[2:16, :]).then_inc(S.ld, 16)
+    g.sync.dma_start(T.D[112:128, 4:8], T.want[0:2, :]).then_inc(S.ld, 16)
+    g.sync.dma_start(T.x0[:, :], T.x[:, :]).then_inc(S.lx, 16)
     for h in range(4):
         g.sync.dma_start(T.Lw[16 * h:16 * h + 16, :], T.want[:, :]).then_inc(S.lw, 16)
-    g.sync.dma_start(T.x0[:, :], T.x[:, :]).then_inc(S.lx, 16)
     g.sync.dma_start(T.wt[:, :], T.w[:, :]).then_inc(S.lv, 16)
 
-    need("v", ("ld", 64))
-    kDc = done("v", V.tensor_scalar(T.Dc[:, :], T.D[:, :], BIG, None, A.mult))
-    need("v", kEO)
-    kXv = done("v", V.tensor_scalar(T.X[:, 0:320], T.D[:, 0:16].indirect(T.EO[:, 0:20]), BIG, None, A.mult))
-    need("s", kDc, kEO)
-    kXs = done("s", Sc.activation(T.X[:, 320:512], T.Dc[:, 0:16].indirect(T.EO[:, 20:32]), F.Copy))
-    need("s", kBt, kRow)
-    kTri = done("s", Sc.activation(T.MK[:, 0:128], T.row[:, :], F.Relu, bias=T.bt[:, 0:1], scale=-BIG))
-    for e in range(4):
-        h = slice(32 * e, 32 * e + 32)
-        kCb = done("s", Sc.activation(T.Cb[h, :], T.Dc[h, e:16:4], F.Copy))
-    need("v", kXv, kXs)
-    kR1 = done("v", V.transpose(T.R[:, 256:512], T.X[:, 256:512]))
-    kR0 = done("v", V.transpose(T.R[:, 0:256], T.X[:, 0:256]))
-    E = [T.E0, T.E1, T.E2, T.E3]
-    need("s", kR1, kCb)
-    kS, kE = {}, {}
-    for k in (3, 2, 1, 0):
-        lo = max(128 * k, 256)
-        kS[k] = done("s", Sc.activation(E[k][:, lo - 128 * k:512 - 128 * k], T.R[:, lo:512], F.Abs, bias=T.Cb[:, k:k + 1], scale=-1.0))
-    kC = done("s", Sc.activation(T.Cf[:, :], T.Cb[:, :], F.Copy, scale=1.0 / BIG))
-    need("s", kP4f)
-    kGsh = done("s", Sc.activation(T.gsh[:, :], T.p4f[:, :], F.Identity, bias=4096.0, scale=-512.0))
-    kT2 = done("s", Sc.activation(T.t2[:, :], T.p4f[:, :], F.Identity, bias=0.5, scale=-16.0))
-    need("v", kR0, kCb)
-    for k in (1, 0):
-        kE[k] = done("v", V.tensor_scalar(E[k][:, 0:256 - 128 * k], T.R[:, 128 * k:256], T.Cb[:, k:k + 1], BIG, A.not_equal, A.mult))
-    need("v", kTri, kMz)
-    for k in (3, 2, 1, 0):
-        need("v", kS[k])
-        if k < 2:
-            need("v", kE[k])
-        kN = done("v", V.tensor_tensor_scan(T.NB[:, 640 * k:512 * k + 512], E[k][:, :], T.MK[:, 0:512 - 128 * k], BIG, A.min, A.max))
-    need("v", kN, kDid, kC)
-    kK = done("v", V.tensor_tensor(T.K[:, :], T.did[:, :], T.NB[:, 511:2048:512], A.subtract))
+    kPid = done("g", g.iota(T.pid[:, :], [[0, 4]], 0, 1))
+    kK16 = iota(T.k16[:, :], 4, 0, 0, 16)
+    kEi = done("g", g.iota(T.Ei[:, :], [[1, 4], [4, 2]], 0, 0))
+    kRow = iota(T.row[:, :], 64, step=-int(BIG))
+    kZero = iota(T.zero[:, :], 64, step=0)
+    iota(T.CW[:, 0:16], 16, step=0)
+    kCz = iota(T.CW[:, 528:544], 16, step=0)
+    kPad4 = iota(T.SRC[:, SE + 3:SE + 4], 1, step=0)
+    done("v", V.memset(T.sgn[lower, :], 1.0))
+    kSgn = done("v", V.memset(T.sgn[upper, :], -1.0))
+    kOnes = done("v", V.memset(T.ones[:, :], 1.0))
+    need("v", kPid)
+    kPm = done("v", V.tensor_scalar(T.pm[:, :], T.pid[:, :], 15, None, A.bitwise_and))
+    kP43 = done("v", V.tensor_scalar(T.p43[:, :], T.pid[:, 0:1], 4, 3, A.arith_shift_right, A.bitwise_and))
+    need("v", kPm, kP43, kK16)
+    kN = done("v", V.tensor_tensor(T.n[:, :], T.pm[:, :], T.k16[:, :], A.add))
+    kGsh = done("v", V.tensor_scalar(T.gsh[:, :], T.p43[:, :], -512.0, WA - UP, A.mult, A.add))
+    need("v", kEi)
+    kEO = done("v", V.tensor_copy(T.EO[:, :], T.Ei[:, :]))
+    need("v", kN, kGsh)
+    done("v", V.tensor_scalar(T.am[:, :], T.n[:, :], 1.0, BIG, A.add, A.mult))
+    kId = done("v", V.tensor_scalar(T.idn[:, :], T.n[:, :], 16.0, T.gsh[:, 0:1], A.mult, A.add))
+    need("s", kSgn, kOnes)
+    for lo in (WA, WB):
+        kWin = done("s", Sc.activation(T.Win[:, lo:lo + 512], T.ones[:, :], F.Identity, scale=T.sgn[:, 0:1]))
+    need("v", kId, kRow)
+    for k in range(4):
+        kMK = done("v", V.tensor_scalar(T.MK[:, 64 * k:64 * k + 64], T.row[:, :], T.am[:, k:k + 1], T.idn[:, k:k + 1], A.add, A.max))
+
+    need("v", ("ld", 48), kEO)
+    kX = done("v", V.tensor_scalar(T.X[:, :], T.D[:, 0:8].indirect(T.EO[:, 0:8]), UP, BIG, A.add, A.mult))
+    need("v", kX)
+    kR = done("v", V.transpose(T.R[:, :], T.X[:, :]))
+    need("s", kX, kGsh)
+    kC = done("s", Sc.activation(T.Cf[:, :], T.X[:, 0:128:16], F.Identity, bias=T.gsh[:, 0:1], scale=1.0 / BIG))
+    need("v", kR)
+    need("s", kR)
+    kE = {}
+    for k in range(8):
+        ops = T.E[:, 64 * k:64 * k + 64], T.R[:, 64 * (k // 4):64 * (k // 4) + 64]
+        own = T.X[:, 16 * k:16 * k + 1]
+        if k in (4, 5, 6):
+            kE[k] = done("s", Sc.activation(*ops, F.Abs, bias=own, scale=-1.0))
+        else:
+            kE[k] = done("v", V.tensor_scalar(*ops, own, BIG, A.not_equal, A.mult))
+    for u in range(2):
+        need("v", kMK, *[kE[k] for k in range(4 * u, 4 * u + 4)])
+        kNB = done("v", V.tensor_tensor_scan(T.NB[:, 256 * u:256 * u + 256], T.E[:, 256 * u:256 * u + 256], T.MK[:, :], BIG, A.min, A.max))
+    need("v", kNB, kC)
+    kK = done("v", V.tensor_tensor(T.K[:, :], T.NB[:, 63:512:64], T.Cf[:, :], A.min))
     need("v", kK)
-    e1 = done("v", V.tensor_tensor(T.G[:, 0:4], T.K[:, :], T.Cf[:, :], A.max))
-    e2 = done("v", V.tensor_tensor(T.G[:, 12:16], T.K[:, :], T.Cf[:, :], A.max))
-    need("v", e1)
-    need("s", e1)
-    done("v", V.tensor_copy(T.G[0:64, 4:8], T.G[64:128, 0:4]))
-    a1 = done("v", V.tensor_copy(T.G[0:64, 8:12], T.G[64:128, 0:4]))
-    done("s", Sc.activation(T.G[64:128, 4:8], T.G[0:64, 0:4], F.Copy))
-    b1 = done("s", Sc.activation(T.G[64:128, 8:12], T.G[0:64, 0:4], F.Copy))
-    need("v", a1, b1, e2)
-    need("s", a1, b1, e2)
-    done("v", V.tensor_copy(T.G[0:32, 16:32], T.G[32:64, 0:16]))
-    done("v", V.tensor_copy(T.G[32:64, 16:32], T.G[0:32, 0:16]))
-    a2 = done("v", V.tensor_copy(T.G[:, 32:40], T.G[:, 0:8]))
-    done("s", Sc.activation(T.G[64:96, 16:32], T.G[96:128, 0:16], F.Copy))
-    b2 = done("s", Sc.activation(T.G[96:128, 16:32], T.G[64:96, 0:16], F.Copy))
-    need("s", kT2, kK16)
-    kThr = done("s", Sc.activation(T.thr[:, :], T.k16[:, :], F.Identity, bias=T.t2[:, 0:1]))
-    need("v", a2, b2)
-    kTG = done("v", V.transpose(T.TG[:, :], T.G[:, 8:40]))
-    need("v", kTG, kGsh)
-    done("v", V.tensor_scalar(T.off1[0:64, :], T.TG[0:64, 0:16], T.gsh[0:64, 0:1], None, A.add))
-    kO1 = done("v", V.tensor_scalar(T.off1[64:128, :], T.TG[64:128, 16:32], T.gsh[64:128, 0:1], None, A.add))
-    need("v", kO1, kOnes, kWin2, ("lz", 32))
-    kSc = done("v", V.tensor_copy(T.Win[:, 0:8704].indirect(T.off1[:, 0:16]), T.ones[:, :]))
+    need("s", kK)
+    kOa = done("v", V.tensor_copy(T.off1[:, 0:8], T.K[:, :]))
+    for e in range(4):
+        kK2 = done("s", Sc.activation(T.K2[quad[e], :], T.K[quad[(e + 1) % 4], :], F.Identity, bias=1024.0 * (-1) ** e))
+    need("v", kOa, kZero, kWin)
+    for u in range(4):
+        if u == 2:
+            need("v", kK2)
+            kOb = done("v", V.tensor_copy(T.off1[:, 8:16], T.K2[:, :]))
+            need("v", kOb)
+        if u:
+            need("v", kSc)
+        kSc = done("v", V.tensor_copy(T.Win[:, :].indirect(T.off1[:, 4 * u:4 * u + 4]), T.zero[:, :]))
     need("v", kSc)
-    need("s", kSc)
-    done("v", V.tensor_copy(T.OB[0:64, :], T.Win[64:128, 2048:2560]))
-    o1 = done("v", V.tensor_copy(T.OB[64:128, 0:160], T.Win[0:64, 6144:6304]))
-    o2 = done("s", Sc.activation(T.OB[64:128, 160:512], T.Win[0:64, 6304:6656], F.Copy))
-    need("v", o1, o2)
-    kCum = done("v", V.tensor_tensor_scan(T.CW[:, 16:528], T.Win[:, 4096:4608], T.OB[:, :], 0.0, A.add, A.add))
+    done("v", V.tensor_tensor_scan(T.M[lower, :], T.Win[lower, WA:WA + 512], T.Win[upper, WA:WA + 512], 0.0, A.max, A.mult))
+    kM = done("v", V.tensor_tensor_scan(T.M[upper, :], T.Win[lower, WB:WB + 512], T.Win[upper, WB:WB + 512], 0.0, A.max, A.mult))
+    need("v", kM)
+    kCum = done("v", V.tensor_tensor_scan(T.CW[:, 16:528], T.M[:, :], T.ones[:, :], 0.0, A.add, A.add))
+    need("s", kN)
+    kThr = done("s", Sc.activation(T.thr[:, :], T.n[:, :], F.Identity, bias=0.5))
+    need("s", ("lx", 16))
+    for t in (2, 3):
+        kPlS = done("s", Sc.activation(T.XP[:, PL * t:PL * t + 512], T.x0[:, t:2048:4], F.Copy))
+    cum = 16
     need("s", kCum, kThr)
-    done("s", Sc.activation(T.J0[:, :], T.CW[:, 16:528], F.Sign, bias=T.thr[:, 0:1], scale=-1.0, accum_out=T.LR[:, 28:29]))
-    c1 = done("s", Sc.activation(T.J1[:, :], T.CW[:, 16:528], F.Sign, bias=T.thr[:, 1:2], scale=-1.0, accum_out=T.LR[:, 29:30]))
+    c1 = done("s", Sc.activation(T.J1[:, :], T.CW[:, cum:cum + CS], F.Sign, bias=T.thr[:, 1:2], scale=-1.0, accum_out=T.P1[:, :]))
+    c0 = done("s", Sc.activation(T.J0[:, :], T.CW[:, cum:cum + 512], F.Sign, bias=T.thr[:, 0:1], scale=-1.0, accum_out=T.SRC[:, SE:SE + 1]))
     need("v", kCum, kThr)
-    kJ2 = done("v", V.tensor_scalar(T.J2[:, :], T.CW[:, 16:528], T.thr[:, 2:3], None, A.is_lt))
+    kJ2 = done("v", V.tensor_scalar(T.J2[:, :], T.CW[:, cum:cum + 512], T.thr[:, 2:3], None, A.is_lt))
+    kJ3 = done("v", V.tensor_scalar(T.J3[:, :], T.CW[:, cum + CS:cum + 512], T.thr[:, 1:2], 2.0, A.is_lt, A.mult))
+    h3 = (512 - CS) // 2
     need("v", kJ2)
-    c2 = done("v", V.tensor_reduce(T.LR[:, 30:31], T.J2[:, :], AxisListType.X, A.add))
+    done("v", V.tensor_tensor_scan(T.SRC[:, SE + 2 - 3 * 255:SE + 3:3], T.J2[:, 0:256], T.J2[:, 256:512], 0.0, A.add, A.add))
+    need("v", kJ3, c1)
+    c2 = done("v", V.tensor_tensor_scan(T.SRC[:, SE + 1 - 3 * (h3 - 1):SE + 2:3], T.J3[:, 0:h3], T.J3[:, h3:2 * h3], T.P1[:, 0:1], A.add, A.add))
     sent = [0]
 
     def mask(dst, pick):
@@ -180,49 +176,53 @@ def rank_program(g, core, T, topo):
     def every(i, n):
         return lambda ne: range(i, ne, n)
 
-    need("g", c1, z3, c2)
+    need("g", c0, c2, kPad4)
     to = [T.cores[(r - 1 - i) % N] for i in range(7)]
     g.remote_dma_fused([RemoteDMATransfer(dst_ids=[at(c) for c in to], dma_engine_mask=mask(to[0], every(0, 1)), remote_sem=S.la,
-                                          srcs=[T.LR[:, 28:32]], dsts=[T.LR[:, 4 * i:4 * i + 4] for i in range(7)])], local_sem=S.out)
+                                          srcs=[T.SRC[:, SE:SE + 4]], dsts=[T.LR[:, 4 * i:4 * i + 4] for i in range(7)])], local_sem=S.out)
     nla = 7 * sent[0]
 
+    kP4 = done("v", V.tensor_scalar(T.p4[:, :], T.pid[:, 0:1], 4, None, A.arith_shift_right))
     need("v", ("lw", 64))
-    done("v", V.tensor_copy(T.off0[0:64, :], T.Lw[0:64, :]))
-    kOff0 = done("v", V.tensor_copy(T.off0[64:128, :], T.Lw[0:64, :]))
-    need("v", kOff0)
-    ko1 = done("v", V.tensor_scalar(T.o1[:, :], T.off0[:, :], T.gsh[:, 0:1], 4608.0, A.add, A.min))
+    done("v", V.tensor_copy(T.off0[lower, :], T.Lw[lower, :]))
+    kOff0 = done("v", V.tensor_copy(T.off0[upper, :], T.Lw[lower, :]))
+    need("v", kP4)
+    kGp = done("v", V.tensor_scalar(T.gp[:, :], T.p4[:, :], -512.0, 4096.0, A.mult, A.add))
+    need("v", c0, c2, kPad4)
+    kOwn = done("v", V.tensor_copy(T.LR[:, 28:32], T.SRC[:, SE:SE + 4]))
+    need("v", kOff0, kGp)
+    ko1 = done("v", V.tensor_scalar(T.o1[:, :], T.off0[:, :], T.gp[:, 0:1], 4608.0, A.add, A.min))
     kq0 = done("v", V.tensor_copy(T.q0[:, :], T.off0[:, :]))
     need("v", ko1)
     done("v", V.tensor_scalar(T.OP[:, 0:64:2], T.o1[:, :], 4095.0, -4080.0, A.max, A.add))
     kOP = done("v", V.tensor_scalar(T.OP[:, 1:64:2], T.o1[:, :], 4095.0, -4080.0, A.max, A.add))
     need("v", ("lx", 16))
-    for t in (0, 1, 2):
+    for t in (0, 1):
         done("v", V.tensor_copy(T.XP[:, PL * t:PL * t + 512], T.x0[:, t:2048:4]))
     kPad = done("v", V.memset(T.XP[:, 512:4 * PL:PL], 0.0))
-    need("s", ("lx", 16))
-    kPlS = done("s", Sc.activation(T.XP[:, PL * 3:PL * 3 + 512], T.x0[:, 3:2048:4], F.Copy))
     need("s", kOP, kCz, kCum)
     kPs = done("s", Sc.activation(T.Pr[:, 384:1024], T.CW[:, 0:544].indirect(T.OP[:, 24:64]), F.Copy))
     need("v", kOP, kCz, kCum)
     kPv = done("v", V.tensor_copy(T.Pr[:, 0:384], T.CW[:, 0:544].indirect(T.OP[:, 0:24])))
 
     a, b = divmod(r, 2)
-    ra = slice(32 * a, 32 * a + 32)
-    need("v", ("la", nla), c1, c2)
+    ra = quad[a]
+    both = slice(0, 32)
+    need("v", ("la", nla), kOwn)
     kX1 = done("v", V.transpose(T.X1[ra, :], T.LR[ra, :]))
     need("v", kX1)
     kXd = done("v", V.tensor_copy(T.X1[ra, 16 - 16 * b:32 - 16 * b], T.X1[ra, 16 * b:16 * b + 16]))
     need("v", kXd)
     need("s", kXd)
-    todo = [slice(32 * d, 32 * d + 32) for d in range(4) if d != a]
-    kcs = done("s", Sc.activation(T.X1[todo[0], :], T.X1[ra, :], F.Copy))
+    todo = [quad[d] for d in range(4) if d != a]
+    kcs = done("s", Sc.activation(T.X1[todo[0], both], T.X1[ra, both], F.Copy))
     for o in todo[1:]:
-        kcv = done("v", V.tensor_copy(T.X1[o, :], T.X1[ra, :]))
+        kcv = done("v", V.tensor_copy(T.X1[o, both], T.X1[ra, both]))
     need("v", kcs, kcv)
-    kX3 = done("v", V.transpose(T.X3[:, :], T.X1[:, :]))
+    kX3 = done("v", V.transpose(T.X3[:, :], T.X1[:, both]))
     need("v", kX3)
     done("v", V.tensor_scalar(T.O[:, 0:21:3], T.X3[:, 0:28:4], 0.5, 256.0, A.mult, A.add))
-    done("v", V.tensor_scalar(T.O[:, 1:21:3], T.X3[:, 1:28:4], 0.5, 256.0, A.mult, A.add))
+    done("v", V.tensor_scalar(T.O[:, 1:21:3], T.X3[:, 1:28:4], 0.5, CS / 2, A.mult, A.add))
     kO = done("v", V.tensor_copy(T.O[:, 2:21:3], T.X3[:, 2:28:4]))
 
     def pick(h, o, t, lo, hi):
@@ -251,7 +251,8 @@ def rank_program(g, core, T, topo):
         sem = S["a%d" % n]
         fused([(d, q[:, c].bitcast(dt.uint8), T.CR[:, e].bitcast(dt.uint8), sem, m) for (d, c, e), m in zip(to, eng[len(to)])])
         fused([(d, p[:, c], T.SR[:, e], sem, m) for (d, c, e), m in zip(to, flip[len(to)])])
-    done("v", V.tensor_scalar(T.OO[:, 0:2], T.X3[:, 28:30], 0.5, 256.0, A.mult, A.add))
+    done("v", V.tensor_scalar(T.OO[:, 0:1], T.X3[:, 28:29], 0.5, 256.0, A.mult, A.add))
+    done("v", V.tensor_scalar(T.OO[:, 1:2], T.X3[:, 29:30], 0.5, CS / 2, A.mult, A.add))
     kOO = done("v", V.tensor_copy(T.OO[:, 2:3], T.X3[:, 30:31]))
     need("s", kOO)
     for t in range(4):
@@ -268,8 +269,8 @@ def rank_program(g, core, T, topo):
     kxa = done("v", V.tensor_tensor(T.xa[:, :], T.PT[:, 0:1024:32], T.PT[:, 16:1024:32], A.add))
     need("v", kxa)
     need("s", kxa)
-    x1 = done("v", V.tensor_copy(T.xb[0:64, :], T.xa[64:128, :]))
-    x2 = done("s", Sc.activation(T.xb[64:128, :], T.xa[0:64, :], F.Copy))
+    x1 = done("v", V.tensor_copy(T.xb[lower, :], T.xa[upper, :]))
+    x2 = done("s", Sc.activation(T.xb[upper, :], T.xa[lower, :], F.Copy))
     need("v", kq1)
     kq2 = done("v", V.tensor_scalar(T.q2[:, :], T.q1[:, :], -1.0, float(r + 7), A.mult, A.add))
     need("v", kHo, kHz)
@@ -318,4 +319,4 @@ def rank_program(g, core, T, topo):
         queues[qn].dma_start(T.y[:, 256 + 16 * lo:256 + 16 * hi], T.ys[:, 16 * lo:16 * hi]).then_inc(S.ly, 16)
 
     need("g", ("out", sent[0]), ("v", cnt["v"]), ("s", cnt["s"]), ("g", cnt["g"]), ("t", cnt["t"]))
-    need("g", ("ld", 64), ("lz", 32), ("lw", 64), ("lx", 16), ("lv", 16), ("ly", 64), ("la", nla), ("a0", 32), ("a1", 32), ("a2", 32))
+    need("g", ("ld", 48), ("lw", 64), ("lx", 16), ("lv", 16), ("ly", 64), ("la", nla), ("a0", 32), ("a1", 32), ("a2", 32))

@@ -1,5 +1,5 @@
 from concourse.bass import DstId, RemoteDMATransfer
-from concourse.mybir import dt, AluOpType, AxisListType, ActivationFunctionType
+from concourse.mybir import dt, AluOpType, ActivationFunctionType
 
 A = AluOpType
 F = ActivationFunctionType
@@ -17,14 +17,15 @@ def sb(kind, **widths):
 
 
 SCRATCH = {
-    **sb("int32", Lw=32, D=8, Ei=8, pid=4, pm=4, p4=1, p43=1, q0=32, q1=32, q2=32, q3=32),
-    **sb("uint16", off0=32, EO=8, off1=16, O=24, OO=4, OP=64, FO=32),
+    **sb("int32", Lw=32, D=8, Ei=8, pid=4, pm=4, p4=1, p43=1),
+    **sb("uint16", EO=8, off1=16, O=24, OP=64, FO=32),
     **sb("float32", Cf=8, X=128, R=128, row=64, sgn=1, gsh=1, gp=1, k16=4, n=4, am=4, idn=4, thr=4, K=8, K2=8, P1=1, SRC=SE + 4,
-         J0=512, J1=CS, LR=32, X1=32, X3=32, Z=384, yv=256, ys=256, o1=32, q4=32, xa=32, xb=32, xc=32, xd=32, xe=32, xf=32),
-    **sb("bfloat16", E=512, NB=512, MK=256, ones=512, zero=64, Win=6656, M=512, CW=544, J2=512, J3=512 - CS,
-         x0=2048, XP=4 * PL, wt=512, H=1344, HO=512, Pr=1024, PT=1024),
-    **sb("float8_e4m3fn_x4", Q=256, Q2=128, QO=128, QW=128, CR=336),
-    **sb("uint8", SQ=256, S2=128, SO=128, SW=128, SR=336),
+         J0=512, J1=CS, LR=32, X1=32, Z=384, yv=256, ys=256, o0=32, xa=32, xc=32, xd=32),
+    **sb("bfloat16", E=512, NB=512, MK=256, ones=512, zero=64, Win=6656, M=512, CW=576, Pl=32, J2=512, J3=514 - CS,
+         x0=2048, XP=4 * PL, wt=512, H=1536, Pr=1024, PT=1024),
+    **sb("float8_e4m3fn_x4", Q=384, QW=128, CR=336),
+    **sb("uint8", SQ=384, SW=128, SR=336),
+    "X3": ("sbuf", [128, 8, 4], "float32"),
     "pa": ("psum", [128, 512], "float32"), "pb": ("psum", [128, 512], "float32"), "po": ("psum", [128, 512], "float32"),
 }
 SEMAPHORES = ["v", "s", "g", "t", "ld", "lw", "lx", "lv", "ly", "la", "a0", "a1", "a2", "out"]
@@ -51,6 +52,14 @@ def rank_program(g, core, T, topo):
         cnt[qn] += 1
         return (qn, cnt[qn])
 
+    def peer(a, i):
+        near = [k for k in range(N) if topo.die(T.cores[k]) == topo.die(T.cores[a])]
+        far = [k for k in range(N) if k not in near]
+        j = near.index(a) + i // 2
+        return near[(j + 1) % len(near)] if i % 2 else far[j % len(far)]
+
+    place = {q: i for q in range(N) for i in range(N) if peer(q, i) == r}
+
     V, Sc = g.vector, g.scalar
     lower, upper = slice(0, 64), slice(64, 128)
     quad = [slice(32 * e, 32 * e + 32) for e in range(4)]
@@ -66,39 +75,47 @@ def rank_program(g, core, T, topo):
         g.sync.dma_start(T.Lw[16 * h:16 * h + 16, :], T.want[:, :]).then_inc(S.lw, 16)
     g.sync.dma_start(T.wt[:, :], T.w[:, :]).then_inc(S.lv, 16)
 
+    h3 = (512 - CS) // 2 + 1
     kPid = done("g", g.iota(T.pid[:, :], [[0, 4]], 0, 1))
     kK16 = iota(T.k16[:, :], 4, 0, 0, 16)
     kEi = done("g", g.iota(T.Ei[:, :], [[1, 4], [4, 2]], 0, 0))
     kRow = iota(T.row[:, :], 64, step=-int(BIG))
     kZero = iota(T.zero[:, :], 64, step=0)
-    iota(T.CW[:, 0:16], 16, step=0)
-    kCz = iota(T.CW[:, 528:544], 16, step=0)
+    kJe = iota(T.J3[:, 0:2 * h3:2 * h3 - 1], 2, CS - 512, 0, 512 - CS)
     kPad4 = iota(T.SRC[:, SE + 3:SE + 4], 1, step=0)
-    done("v", V.memset(T.sgn[lower, :], 1.0))
-    kSgn = done("v", V.memset(T.sgn[upper, :], -1.0))
+    for e in range(4):
+        lo, hi = place[2 * e], place[2 * e + 1]
+        need("g", ("g", cnt["g"]))
+        kPl = done("g", g.iota(T.Pl[quad[e], :], [[CAP * (lo - hi), 2], [0, 16]], -CAP * lo, 0, allow_small_or_imprecise_dtypes=True))
     kOnes = done("v", V.memset(T.ones[:, :], 1.0))
     need("v", kPid)
     kPm = done("v", V.tensor_scalar(T.pm[:, :], T.pid[:, :], 15, None, A.bitwise_and))
     kP43 = done("v", V.tensor_scalar(T.p43[:, :], T.pid[:, 0:1], 4, 3, A.arith_shift_right, A.bitwise_and))
-    need("v", kPm, kP43, kK16)
+    done("v", V.memset(T.sgn[lower, :], 1.0))
+    kSgn = done("v", V.memset(T.sgn[upper, :], -1.0))
+    need("v", kPm, kP43, kK16, kEi)
     kN = done("v", V.tensor_tensor(T.n[:, :], T.pm[:, :], T.k16[:, :], A.add))
     kGsh = done("v", V.tensor_scalar(T.gsh[:, :], T.p43[:, :], -512.0, WA - UP, A.mult, A.add))
-    need("v", kEi)
     kEO = done("v", V.tensor_copy(T.EO[:, :], T.Ei[:, :]))
     need("v", kN, kGsh)
     done("v", V.tensor_scalar(T.am[:, :], T.n[:, :], 1.0, BIG, A.add, A.mult))
     kId = done("v", V.tensor_scalar(T.idn[:, :], T.n[:, :], 16.0, T.gsh[:, 0:1], A.mult, A.add))
-    need("s", kSgn, kOnes)
-    for lo in (WA, WB):
-        kWin = done("s", Sc.activation(T.Win[:, lo:lo + 512], T.ones[:, :], F.Identity, scale=T.sgn[:, 0:1]))
-    need("v", kId, kRow)
-    for k in range(4):
-        kMK = done("v", V.tensor_scalar(T.MK[:, 64 * k:64 * k + 64], T.row[:, :], T.am[:, k:k + 1], T.idn[:, k:k + 1], A.add, A.max))
 
+    def window(lo):
+        need("s", kSgn, kOnes)
+        return done("s", Sc.activation(T.Win[:, lo:lo + 512], T.ones[:, :], F.Identity, scale=T.sgn[:, 0:1]))
+
+    def entry_mask(k):
+        need("v", kId, kRow)
+        return done("v", V.tensor_scalar(T.MK[:, 64 * k:64 * k + 64], T.row[:, :], T.am[:, k:k + 1], T.idn[:, k:k + 1], A.add, A.max))
+
+    window(WA)
     need("v", ("ld", 48), kEO)
     kX = done("v", V.tensor_scalar(T.X[:, :], T.D[:, 0:8].indirect(T.EO[:, 0:8]), UP, BIG, A.add, A.mult))
+    entry_mask(0)
     need("v", kX)
     kR = done("v", V.transpose(T.R[:, :], T.X[:, :]))
+    entry_mask(1)
     need("s", kX, kGsh)
     kC = done("s", Sc.activation(T.Cf[:, :], T.X[:, 0:128:16], F.Identity, bias=T.gsh[:, 0:1], scale=1.0 / BIG))
     need("v", kR)
@@ -107,10 +124,13 @@ def rank_program(g, core, T, topo):
     for k in range(8):
         ops = T.E[:, 64 * k:64 * k + 64], T.R[:, 64 * (k // 4):64 * (k // 4) + 64]
         own = T.X[:, 16 * k:16 * k + 1]
-        if k in (4, 5, 6):
+        if k >= 4:
             kE[k] = done("s", Sc.activation(*ops, F.Abs, bias=own, scale=-1.0))
         else:
             kE[k] = done("v", V.tensor_scalar(*ops, own, BIG, A.not_equal, A.mult))
+    entry_mask(2)
+    kMK = entry_mask(3)
+    kWin = window(WB)
     for u in range(2):
         need("v", kMK, *[kE[k] for k in range(4 * u, 4 * u + 4)])
         kNB = done("v", V.tensor_tensor_scan(T.NB[:, 256 * u:256 * u + 256], T.E[:, 256 * u:256 * u + 256], T.MK[:, :], BIG, A.min, A.max))
@@ -123,9 +143,10 @@ def rank_program(g, core, T, topo):
         kK2 = done("s", Sc.activation(T.K2[quad[e], :], T.K[quad[(e + 1) % 4], :], F.Identity, bias=1024.0 * (-1) ** e))
     need("v", kOa, kZero, kWin)
     for u in range(4):
-        if u == 2:
+        if u == 1:
             need("v", kK2)
             kOb = done("v", V.tensor_copy(T.off1[:, 8:16], T.K2[:, :]))
+        if u == 2:
             need("v", kOb)
         if u:
             need("v", kSc)
@@ -134,23 +155,22 @@ def rank_program(g, core, T, topo):
     done("v", V.tensor_tensor_scan(T.M[lower, :], T.Win[lower, WA:WA + 512], T.Win[upper, WA:WA + 512], 0.0, A.max, A.mult))
     kM = done("v", V.tensor_tensor_scan(T.M[upper, :], T.Win[lower, WB:WB + 512], T.Win[upper, WB:WB + 512], 0.0, A.max, A.mult))
     need("v", kM)
-    kCum = done("v", V.tensor_tensor_scan(T.CW[:, 16:528], T.M[:, :], T.ones[:, :], 0.0, A.add, A.add))
+    cum = 32
+    kCum = done("v", V.tensor_tensor_scan(T.CW[:, cum:cum + 512], T.M[:, :], T.ones[:, :], 0.0, A.add, A.add))
     need("s", kN)
     kThr = done("s", Sc.activation(T.thr[:, :], T.n[:, :], F.Identity, bias=0.5))
     need("s", ("lx", 16))
     for t in (2, 3):
         kPlS = done("s", Sc.activation(T.XP[:, PL * t:PL * t + 512], T.x0[:, t:2048:4], F.Copy))
-    cum = 16
     need("s", kCum, kThr)
     c1 = done("s", Sc.activation(T.J1[:, :], T.CW[:, cum:cum + CS], F.Sign, bias=T.thr[:, 1:2], scale=-1.0, accum_out=T.P1[:, :]))
     c0 = done("s", Sc.activation(T.J0[:, :], T.CW[:, cum:cum + 512], F.Sign, bias=T.thr[:, 0:1], scale=-1.0, accum_out=T.SRC[:, SE:SE + 1]))
     need("v", kCum, kThr)
-    kJ2 = done("v", V.tensor_scalar(T.J2[:, :], T.CW[:, cum:cum + 512], T.thr[:, 2:3], None, A.is_lt))
-    kJ3 = done("v", V.tensor_scalar(T.J3[:, :], T.CW[:, cum + CS:cum + 512], T.thr[:, 1:2], 2.0, A.is_lt, A.mult))
-    h3 = (512 - CS) // 2
+    kJ2 = done("v", V.tensor_scalar(T.J2[:, :], T.CW[:, cum:cum + 512], T.thr[:, 2:3], 2.0, A.is_lt, A.mult))
+    kJ3 = done("v", V.tensor_scalar(T.J3[:, 1:2 * h3 - 1], T.CW[:, cum + CS:cum + 512], T.thr[:, 1:2], 2.0, A.is_lt, A.mult))
     need("v", kJ2)
-    done("v", V.tensor_tensor_scan(T.SRC[:, SE + 2 - 3 * 255:SE + 3:3], T.J2[:, 0:256], T.J2[:, 256:512], 0.0, A.add, A.add))
-    need("v", kJ3, c1)
+    done("v", V.tensor_tensor_scan(T.SRC[:, SE + 2 - 3 * 255:SE + 3:3], T.J2[:, 0:256], T.J2[:, 256:512], -512.0, A.add, A.add))
+    need("v", kJ3, c1, kJe)
     c2 = done("v", V.tensor_tensor_scan(T.SRC[:, SE + 1 - 3 * (h3 - 1):SE + 2:3], T.J3[:, 0:h3], T.J3[:, h3:2 * h3], T.P1[:, 0:1], A.add, A.add))
     sent = [0]
 
@@ -177,137 +197,99 @@ def rank_program(g, core, T, topo):
         return lambda ne: range(i, ne, n)
 
     need("g", c0, c2, kPad4)
-    to = [T.cores[(r - 1 - i) % N] for i in range(7)]
+    to = [T.cores[q] for q in sorted(place, key=place.get)[:7]]
     g.remote_dma_fused([RemoteDMATransfer(dst_ids=[at(c) for c in to], dma_engine_mask=mask(to[0], every(0, 1)), remote_sem=S.la,
                                           srcs=[T.SRC[:, SE:SE + 4]], dsts=[T.LR[:, 4 * i:4 * i + 4] for i in range(7)])], local_sem=S.out)
     nla = 7 * sent[0]
 
     kP4 = done("v", V.tensor_scalar(T.p4[:, :], T.pid[:, 0:1], 4, None, A.arith_shift_right))
     need("v", ("lw", 64))
-    done("v", V.tensor_copy(T.off0[lower, :], T.Lw[lower, :]))
-    kOff0 = done("v", V.tensor_copy(T.off0[upper, :], T.Lw[lower, :]))
+    done("v", V.tensor_copy(T.o0[lower, :], T.Lw[lower, :]))
+    kOff0 = done("v", V.tensor_copy(T.o0[upper, :], T.Lw[lower, :]))
     need("v", kP4)
-    kGp = done("v", V.tensor_scalar(T.gp[:, :], T.p4[:, :], -512.0, 4096.0, A.mult, A.add))
+    kGp = done("v", V.tensor_scalar(T.gp[:, :], T.p4[:, :], -512.0, float(cum), A.mult, A.add))
+    need("v", kPl)
+    for lo in (0, cum + 512):
+        kCz = done("v", V.transpose(T.CW[:, lo:lo + 32], T.Pl[:, :]))
+    need("v", kOff0, kGp)
+    for u in range(2):
+        kOP = done("v", V.tensor_scalar(T.OP[:, u:64:2], T.o0[:, :], T.gp[:, 0:1], cum + 512.0, A.add, A.min))
     need("v", c0, c2, kPad4)
     kOwn = done("v", V.tensor_copy(T.LR[:, 28:32], T.SRC[:, SE:SE + 4]))
-    need("v", kOff0, kGp)
-    ko1 = done("v", V.tensor_scalar(T.o1[:, :], T.off0[:, :], T.gp[:, 0:1], 4608.0, A.add, A.min))
-    kq0 = done("v", V.tensor_copy(T.q0[:, :], T.off0[:, :]))
-    need("v", ko1)
-    done("v", V.tensor_scalar(T.OP[:, 0:64:2], T.o1[:, :], 4095.0, -4080.0, A.max, A.add))
-    kOP = done("v", V.tensor_scalar(T.OP[:, 1:64:2], T.o1[:, :], 4095.0, -4080.0, A.max, A.add))
     need("v", ("lx", 16))
     for t in (0, 1):
         done("v", V.tensor_copy(T.XP[:, PL * t:PL * t + 512], T.x0[:, t:2048:4]))
     kPad = done("v", V.memset(T.XP[:, 512:4 * PL:PL], 0.0))
     need("s", kOP, kCz, kCum)
-    kPs = done("s", Sc.activation(T.Pr[:, 384:1024], T.CW[:, 0:544].indirect(T.OP[:, 24:64]), F.Copy))
+    kPs = done("s", Sc.activation(T.Pr[:, 384:1024], T.CW[:, :].indirect(T.OP[:, 24:64]), F.Copy))
     need("v", kOP, kCz, kCum)
-    kPv = done("v", V.tensor_copy(T.Pr[:, 0:384], T.CW[:, 0:544].indirect(T.OP[:, 0:24])))
+    kPv = done("v", V.tensor_copy(T.Pr[:, 0:384], T.CW[:, :].indirect(T.OP[:, 0:24])))
 
     a, b = divmod(r, 2)
     ra = quad[a]
-    both = slice(0, 32)
     need("v", ("la", nla), kOwn)
     kX1 = done("v", V.transpose(T.X1[ra, :], T.LR[ra, :]))
     need("v", kX1)
     kXd = done("v", V.tensor_copy(T.X1[ra, 16 - 16 * b:32 - 16 * b], T.X1[ra, 16 * b:16 * b + 16]))
     need("v", kXd)
-    need("s", kXd)
-    todo = [quad[d] for d in range(4) if d != a]
-    kcs = done("s", Sc.activation(T.X1[todo[0], both], T.X1[ra, both], F.Copy))
-    for o in todo[1:]:
-        kcv = done("v", V.tensor_copy(T.X1[o, both], T.X1[ra, both]))
-    need("v", kcs, kcv)
-    kX3 = done("v", V.transpose(T.X3[:, :], T.X1[:, both]))
+    kX3 = done("v", V.transpose(T.X3[ra, :, :], T.X1[ra, :]))
     need("v", kX3)
-    done("v", V.tensor_scalar(T.O[:, 0:21:3], T.X3[:, 0:28:4], 0.5, 256.0, A.mult, A.add))
-    done("v", V.tensor_scalar(T.O[:, 1:21:3], T.X3[:, 1:28:4], 0.5, CS / 2, A.mult, A.add))
-    kO = done("v", V.tensor_copy(T.O[:, 2:21:3], T.X3[:, 2:28:4]))
+    for o in quad:
+        kO = done("v", V.tensor_scalar(T.O[o, :], T.X3[ra, :, 0:3], 0.5, 256.0, A.mult, A.add))
 
-    def pick(h, o, t, lo, hi):
-        return h[:, 64 * lo + t:64 * hi:4], T.XP[:, PL * t:PL * t + 513].indirect(o[:, lo:hi])
+    def pick(n, t):
+        return T.H[:, 768 * n + t:768 * n + 768:4], T.XP[:, PL * t:PL * t + 513].indirect(T.O[:, 12 * n:12 * n + 12])
 
-    part = [(0, 8), (8, 16), (16, 21)]
     need("s", kO, kPlS, kPad)
     kh = []
-    for lo, hi in part:
+    for n in range(2):
         for t in (2, 3):
-            k = done("s", Sc.activation(*pick(T.H, T.O, t, lo, hi), F.Copy))
+            k = done("s", Sc.activation(*pick(n, t), F.Copy))
         kh.append(k)
     need("v", kO, kPlS, kPad)
-    eng = {2: [every(0, 2), every(1, 2)], 3: [every(0, 2), every(1, 4), every(3, 4)]}
-    flip = {2: [every(1, 2), every(0, 2)], 3: [every(1, 2), every(0, 4), every(2, 4)]}
-    kv = {}
-    for n, ids in enumerate(((0, 1), (2, 3, 4), (5, 6))):
-        for m, t in ((n, 0), (n, 1), (n + 1, 0)):
-            if m < 3 and (m, t) not in kv:
-                kv[m, t] = done("v", V.tensor_copy(*pick(T.H, T.O, t, *part[m])))
-        q, p, lo, c0 = (T.Q, T.SQ, 128 * n, 0) if n < 2 else (T.Q2, T.S2, 0, 208)
-        need("v", kv[n, 0], kv[n, 1], kh[n])
-        kq = done("v", V.quantize_mx(q[:, lo:lo + 128], p[:, lo:lo + 128], T.H[:, 4 * (lo + c0):4 * (lo + c0) + 512]))
+    eng = {4: [every(0, 4), every(1, 4), every(2, 4), every(3, 4)], 3: [every(0, 4), every(1, 2), every(2, 4)]}
+    flip = {4: [every(1, 4), every(0, 4), every(3, 4), every(2, 4)], 3: [every(1, 4), every(0, 2), every(3, 4)]}
+    for n, batches in enumerate(([(0, 1, 2, 3)], [(4, 5, 6)])):
+        for t in (0, 1):
+            kv = done("v", V.tensor_copy(*pick(n, t)))
+        need("v", kv, kh[n])
+        kq = done("v", V.quantize_mx(T.Q[:, 192 * n:192 * n + 192], T.SQ[:, 192 * n:192 * n + 192], T.H[:, 768 * n:768 * n + 768]))
         need("g", kq)
-        to = [((r + 1 + i) % N, slice(CAP * i - c0, CAP * i - c0 + CAP), slice(CAP * i, CAP * i + CAP)) for i in ids]
         sem = S["a%d" % n]
-        fused([(d, q[:, c].bitcast(dt.uint8), T.CR[:, e].bitcast(dt.uint8), sem, m) for (d, c, e), m in zip(to, eng[len(to)])])
-        fused([(d, p[:, c], T.SR[:, e], sem, m) for (d, c, e), m in zip(to, flip[len(to)])])
-    done("v", V.tensor_scalar(T.OO[:, 0:1], T.X3[:, 28:29], 0.5, 256.0, A.mult, A.add))
-    done("v", V.tensor_scalar(T.OO[:, 1:2], T.X3[:, 29:30], 0.5, CS / 2, A.mult, A.add))
-    kOO = done("v", V.tensor_copy(T.OO[:, 2:3], T.X3[:, 30:31]))
-    need("s", kOO)
-    for t in range(4):
-        kHo = done("s", Sc.activation(*pick(T.HO, T.OO, t, 0, 3), F.Copy))
+        for ids in batches:
+            to = [(peer(r, i), slice(CAP * i, CAP * i + CAP)) for i in ids]
+            fused([(d, T.Q[:, c].bitcast(dt.uint8), T.CR[:, c].bitcast(dt.uint8), sem, m) for (d, c), m in zip(to, eng[len(to)])])
+            fused([(d, T.SQ[:, c], T.SR[:, c], sem, m) for (d, c), m in zip(to, flip[len(to)])])
     need("v", ("lv", 16))
     kW = done("v", V.quantize_mx(T.QW[:, :], T.SW[:, :], T.wt[:, :]))
 
+    q0 = quad[0]
     need("v", kPs, kPv)
     kPT = done("v", V.transpose(T.PT[:, :], T.Pr[:, :]))
-    kHz = done("v", V.memset(T.HO[:, 192:512], 0.0))
-    need("v", kq0)
-    kq1 = done("v", V.tensor_scalar(T.q1[:, :], T.q0[:, :], 9, None, A.arith_shift_right))
     need("v", kPT)
     kxa = done("v", V.tensor_tensor(T.xa[:, :], T.PT[:, 0:1024:32], T.PT[:, 16:1024:32], A.add))
     need("v", kxa)
-    need("s", kxa)
-    x1 = done("v", V.tensor_copy(T.xb[lower, :], T.xa[upper, :]))
-    x2 = done("s", Sc.activation(T.xb[upper, :], T.xa[lower, :], F.Copy))
-    need("v", kq1)
-    kq2 = done("v", V.tensor_scalar(T.q2[:, :], T.q1[:, :], -1.0, float(r + 7), A.mult, A.add))
-    need("v", kHo, kHz)
-    kqo = done("v", V.quantize_mx(T.QO[:, :], T.SO[:, :], T.HO[:, :]))
-    need("v", x1, x2)
-    kxc = done("v", V.tensor_tensor(T.xc[:, :], T.xa[:, :], T.xb[:, :], A.add))
-    need("v", kq2)
-    kq3 = done("v", V.tensor_scalar(T.q3[:, :], T.q2[:, :], 7, None, A.bitwise_and))
+    kxc = done("v", V.tensor_tensor(T.xc[lower, :], T.xa[lower, :], T.xa[upper, :], A.add))
     need("v", kxc)
-    need("s", kxc)
-    done("v", V.tensor_copy(T.xd[0:32, :], T.xc[32:64, :]))
-    x3 = done("v", V.tensor_copy(T.xd[32:64, :], T.xc[0:32, :]))
-    done("s", Sc.activation(T.xd[64:96, :], T.xc[96:128, :], F.Copy))
-    x4 = done("s", Sc.activation(T.xd[96:128, :], T.xc[64:96, :], F.Copy))
-    need("v", kq3)
-    kq4 = done("v", V.tensor_scalar(T.q4[:, :], T.q3[:, :], 48.0, -1.0, A.mult, A.add))
-    need("v", kq4)
-    kxe = done("v", V.tensor_tensor(T.xe[:, :], T.xc[:, :], T.q4[:, :], A.add))
-    need("v", x3, x4, kxe)
-    kxf = done("v", V.tensor_tensor(T.xf[:, :], T.xe[:, :], T.xd[:, :], A.add))
-    need("v", kxf)
-    kFO = done("v", V.tensor_copy(T.FO[:, :], T.xf[:, :]))
+    kxd = done("v", V.tensor_tensor(T.xd[q0, :], T.xc[q0, :], T.xc[quad[1], :], A.add))
+    need("v", kxd)
+    for o in quad:
+        kFO = done("v", V.tensor_scalar(T.FO[o, :], T.xd[q0, :], CAP * sum(place.values()) - 1.0, None, A.add))
 
     ts = g.tensor
-    need("t", kW, kqo)
-    m0 = done("t", ts.matmul_mx(T.po[:, 0:128], T.QW[:, :], T.SW[:, :], T.QO[:, :], T.SO[:, :], True, True))
-    need("t", ("a0", 32), ("a1", 32))
-    m1 = done("t", ts.matmul_mx(T.pa[:, 0:240], T.QW[:, :], T.SW[:, :], T.CR[:, 0:240], T.SR[:, 0:240], True, True))
-    need("t", ("a2", 32))
-    m2 = done("t", ts.matmul_mx(T.pb[:, 0:128], T.QW[:, :], T.SW[:, :], T.CR[:, 208:336], T.SR[:, 208:336], True, True))
+    need("t", kW, kq)
+    m0 = done("t", ts.matmul_mx(T.po[:, 0:128], T.QW[:, :], T.SW[:, :], T.Q[:, 256:384], T.SQ[:, 256:384], True, True))
+    need("t", ("a0", 32))
+    m1 = done("t", ts.matmul_mx(T.pa[:, 0:192], T.QW[:, :], T.SW[:, :], T.CR[:, 0:192], T.SR[:, 0:192], True, True))
+    need("t", ("a1", 32))
+    m2 = done("t", ts.matmul_mx(T.pb[:, 0:144], T.QW[:, :], T.SW[:, :], T.CR[:, 192:336], T.SR[:, 192:336], True, True))
 
-    need("v", m0)
-    zo = done("v", V.tensor_copy(T.Z[:, 336:384], T.po[:, 0:48]))
+    need("s", m0)
+    zo = done("s", Sc.activation(T.Z[:, 336:384], T.po[:, 80:128], F.Copy))
     need("s", m1)
-    za = done("s", Sc.activation(T.Z[:, 0:240], T.pa[:, 0:240], F.Copy))
+    za = done("s", Sc.activation(T.Z[:, 0:192], T.pa[:, 0:192], F.Copy))
     need("v", m2)
-    zb = done("v", V.tensor_copy(T.Z[:, 240:336], T.pb[:, 32:128]))
+    zb = done("v", V.tensor_copy(T.Z[:, 192:336], T.pb[:, 0:144]))
     need("v", kFO, zo, za, zb)
     need("s", kFO, zo, za, zb)
     for lo, hi, qn in ((0, 6, "y"), (6, 16, "s")):
@@ -319,4 +301,4 @@ def rank_program(g, core, T, topo):
         queues[qn].dma_start(T.y[:, 256 + 16 * lo:256 + 16 * hi], T.ys[:, 16 * lo:16 * hi]).then_inc(S.ly, 16)
 
     need("g", ("out", sent[0]), ("v", cnt["v"]), ("s", cnt["s"]), ("g", cnt["g"]), ("t", cnt["t"]))
-    need("g", ("ld", 48), ("lw", 64), ("lx", 16), ("lv", 16), ("ly", 64), ("la", nla), ("a0", 32), ("a1", 32), ("a2", 32))
+    need("g", ("ld", 48), ("lw", 64), ("lx", 16), ("lv", 16), ("ly", 64), ("la", nla), ("a0", 32), ("a1", 32))

@@ -8,8 +8,11 @@ PL = 528
 BIG = 8192.0
 UP = 1024.0
 WA, WB = 2560, 4608
-CS = 288
+CS = 272
 SE = 768
+BATCHES = [((0, 1, 2, 3), 0, 192, [(0, 12, 0), (0, 12, 1)], [(0, 12, 2), (0, 12, 3)]),
+           ((4, 5, 6), 192, 336, [(12, 21, 0), (12, 18, 1)], [(12, 21, 2), (12, 21, 3), (18, 21, 1)])]
+LAST = 192
 
 
 def sb(kind, **widths):
@@ -17,18 +20,18 @@ def sb(kind, **widths):
 
 
 SCRATCH = {
-    **sb("int32", Lw=32, D=8, Ei=8, pid=4, pm=4, p4=1, p43=1),
+    **sb("int32", Lw=32, D=8, Ei=8, pid=4, pm=4, p43=1),
     **sb("uint16", EO=8, off1=16, O=24, OP=64, FO=32),
-    **sb("float32", Cf=8, X=128, R=128, row=64, sgn=1, gsh=1, gp=1, k16=4, n=4, am=4, idn=4, thr=4, K=8, K2=8, P1=1, SRC=SE + 4,
-         J0=512, J1=CS, LR=32, X1=32, Z=384, yv=256, ys=256, o0=32, xa=32, xc=32, xd=32),
-    **sb("bfloat16", E=512, NB=512, MK=256, ones=512, zero=64, Win=6656, M=512, CW=576, Pl=32, J2=512, J3=514 - CS,
+    **sb("float32", Cf=8, X=128, R=128, gsh=1, gp=1, k16=4, n=4, thr=4, nthr=4, K=8, K2=8, P1=1, SRC=SE + 4,
+         J0=512, J1=CS, LR=32, Z=384, Y=512, xa=32, xc=32, xd=32),
+    **sb("bfloat16", row=260, E=520, NB=520, MK=260, ones=512, zero=64, Win=6656, M=512, CW=576, Pl=32, J2=512, J3=514 - CS,
          x0=2048, XP=4 * PL, wt=512, H=1536, Pr=1024, PT=1024),
-    **sb("float8_e4m3fn_x4", Q=384, QW=128, CR=336),
-    **sb("uint8", SQ=384, SW=128, SR=336),
-    "X3": ("sbuf", [128, 8, 4], "float32"),
+    **sb("float8_e4m3fn_x4", **{"Q%d" % n: b[2] - b[1] for n, b in enumerate(BATCHES)}, QO=128, QW=128, CR=336),
+    **sb("uint8", **{"S%d" % n: b[2] - b[1] for n, b in enumerate(BATCHES)}, SO=128, SW=128, SR=336),
+    "X1": ("sbuf", [128, 2, 32], "float32"), "X3": ("sbuf", [128, 8, 4], "float32"),
     "pa": ("psum", [128, 512], "float32"), "pb": ("psum", [128, 512], "float32"), "po": ("psum", [128, 512], "float32"),
 }
-SEMAPHORES = ["v", "s", "g", "t", "ld", "lw", "lx", "lv", "ly", "la", "a0", "a1", "a2", "out"]
+SEMAPHORES = ["v", "s", "g", "t", "ld", "lw", "lx", "lv", "ly", "la", "out"] + ["a%d" % n for n in range(len(BATCHES))]
 
 
 def rank_program(g, core, T, topo):
@@ -71,103 +74,114 @@ def rank_program(g, core, T, topo):
     g.scalar.dma_start(T.D[0:112, 4:8], T.want[2:16, :]).then_inc(S.ld, 16)
     g.sync.dma_start(T.D[112:128, 4:8], T.want[0:2, :]).then_inc(S.ld, 16)
     g.sync.dma_start(T.x0[:, :], T.x[:, :]).then_inc(S.lx, 16)
-    for h in range(4):
-        g.sync.dma_start(T.Lw[16 * h:16 * h + 16, :], T.want[:, :]).then_inc(S.lw, 16)
     g.sync.dma_start(T.wt[:, :], T.w[:, :]).then_inc(S.lv, 16)
+    for h in range(8):
+        g.sync.dma_start(T.Lw[16 * h:16 * h + 16, :], T.want[:, :]).then_inc(S.lw, 16)
 
     h3 = (512 - CS) // 2 + 1
     kPid = done("g", g.iota(T.pid[:, :], [[0, 4]], 0, 1))
     kK16 = iota(T.k16[:, :], 4, 0, 0, 16)
     kEi = done("g", g.iota(T.Ei[:, :], [[1, 4], [4, 2]], 0, 0))
-    kRow = iota(T.row[:, :], 64, step=-int(BIG))
+    kRow = done("g", g.iota(T.row[:, :], [[-16, 4], [1, 65]], 0, 0, allow_small_or_imprecise_dtypes=True))
+    kEe = iota(T.E[:, 64:520:65], 8, 1, step=0)
     kZero = iota(T.zero[:, :], 64, step=0)
     kJe = iota(T.J3[:, 0:2 * h3:2 * h3 - 1], 2, CS - 512, 0, 512 - CS)
     kPad4 = iota(T.SRC[:, SE + 3:SE + 4], 1, step=0)
     for e in range(4):
         lo, hi = place[2 * e], place[2 * e + 1]
         need("g", ("g", cnt["g"]))
-        kPl = done("g", g.iota(T.Pl[quad[e], :], [[CAP * (lo - hi), 2], [0, 16]], -CAP * lo, 0, allow_small_or_imprecise_dtypes=True))
+        kPl = done("g", g.iota(T.Pl[quad[e], :], [[CAP * (hi - lo), 2], [0, 16]], CAP * lo, 0, allow_small_or_imprecise_dtypes=True))
     kOnes = done("v", V.memset(T.ones[:, :], 1.0))
     need("v", kPid)
     kPm = done("v", V.tensor_scalar(T.pm[:, :], T.pid[:, :], 15, None, A.bitwise_and))
     kP43 = done("v", V.tensor_scalar(T.p43[:, :], T.pid[:, 0:1], 4, 3, A.arith_shift_right, A.bitwise_and))
-    done("v", V.memset(T.sgn[lower, :], 1.0))
-    kSgn = done("v", V.memset(T.sgn[upper, :], -1.0))
-    need("v", kPm, kP43, kK16, kEi)
+    need("v", kPm, kK16)
     kN = done("v", V.tensor_tensor(T.n[:, :], T.pm[:, :], T.k16[:, :], A.add))
-    kGsh = done("v", V.tensor_scalar(T.gsh[:, :], T.p43[:, :], -512.0, WA - UP, A.mult, A.add))
+    need("v", kP43, kEi)
+    kGsh = done("v", V.tensor_scalar(T.gsh[:, :], T.p43[:, :], -512.0 / BIG, (WA - UP) / BIG, A.mult, A.add))
     kEO = done("v", V.tensor_copy(T.EO[:, :], T.Ei[:, :]))
-    need("v", kN, kGsh)
-    done("v", V.tensor_scalar(T.am[:, :], T.n[:, :], 1.0, BIG, A.add, A.mult))
-    kId = done("v", V.tensor_scalar(T.idn[:, :], T.n[:, :], 16.0, T.gsh[:, 0:1], A.mult, A.add))
 
     def window(lo):
-        need("s", kSgn, kOnes)
-        return done("s", Sc.activation(T.Win[:, lo:lo + 512], T.ones[:, :], F.Identity, scale=T.sgn[:, 0:1]))
-
-    def entry_mask(k):
-        need("v", kId, kRow)
-        return done("v", V.tensor_scalar(T.MK[:, 64 * k:64 * k + 64], T.row[:, :], T.am[:, k:k + 1], T.idn[:, k:k + 1], A.add, A.max))
+        need("s", kOnes)
+        return done("s", Sc.activation(T.Win[:, lo:lo + 512], T.ones[:, :], F.Copy, scale=-1.0))
 
     window(WA)
     need("v", ("ld", 48), kEO)
-    kX = done("v", V.tensor_scalar(T.X[:, :], T.D[:, 0:8].indirect(T.EO[:, 0:8]), UP, BIG, A.add, A.mult))
-    entry_mask(0)
+    kX = done("v", V.tensor_scalar(T.X[:, :], T.D[:, 0:8].indirect(T.EO[:, 0:8]), UP, None, A.add))
+    need("v", kN, kRow)
+    kMK = done("v", V.tensor_scalar(T.MK[:, :], T.row[:, :], T.n[:, 0:1], None, A.is_le))
     need("v", kX)
     kR = done("v", V.transpose(T.R[:, :], T.X[:, :]))
-    entry_mask(1)
+    need("v", kMK, kGsh)
+    kMK = done("v", V.tensor_scalar(T.MK[:, 64:260:65], T.n[:, :], 16.0 / BIG, T.gsh[:, 0:1], A.mult, A.add))
     need("s", kX, kGsh)
     kC = done("s", Sc.activation(T.Cf[:, :], T.X[:, 0:128:16], F.Identity, bias=T.gsh[:, 0:1], scale=1.0 / BIG))
     need("v", kR)
     need("s", kR)
     kE = {}
     for k in range(8):
-        ops = T.E[:, 64 * k:64 * k + 64], T.R[:, 64 * (k // 4):64 * (k // 4) + 64]
+        ops = T.E[:, 65 * k:65 * k + 64], T.R[:, 64 * (k // 4):64 * (k // 4) + 64]
         own = T.X[:, 16 * k:16 * k + 1]
-        if k >= 4:
+        if k >= 5:
             kE[k] = done("s", Sc.activation(*ops, F.Abs, bias=own, scale=-1.0))
         else:
-            kE[k] = done("v", V.tensor_scalar(*ops, own, BIG, A.not_equal, A.mult))
-    entry_mask(2)
-    kMK = entry_mask(3)
+            kE[k] = done("v", V.tensor_scalar(*ops, own, None, A.not_equal))
     kWin = window(WB)
+    kNB, kK, kOa, kOb, kK2 = {}, {}, {}, {}, {}
     for u in range(2):
-        need("v", kMK, *[kE[k] for k in range(4 * u, 4 * u + 4)])
-        kNB = done("v", V.tensor_tensor_scan(T.NB[:, 256 * u:256 * u + 256], T.E[:, 256 * u:256 * u + 256], T.MK[:, :], BIG, A.min, A.max))
-    need("v", kNB, kC)
-    kK = done("v", V.tensor_tensor(T.K[:, :], T.NB[:, 63:512:64], T.Cf[:, :], A.min))
-    need("v", kK)
-    need("s", kK)
-    kOa = done("v", V.tensor_copy(T.off1[:, 0:8], T.K[:, :]))
+        need("v", kMK, kEe, *[kE[k] for k in range(4 * u, 4 * u + 4)])
+        kNB[u] = done("v", V.tensor_tensor_scan(T.NB[:, 260 * u:260 * u + 260], T.E[:, 260 * u:260 * u + 260], T.MK[:, :], 1.0, A.min, A.add))
+    for u in range(2):
+        need("v", kNB[u], kC)
+        kK[u] = done("v", V.tensor_tensor(T.K[:, 4 * u:4 * u + 4], T.NB[:, 260 * u + 64:260 * u + 260:65], T.Cf[:, 4 * u:4 * u + 4], A.min))
+    for u in range(2):
+        need("v", kK[u])
+        kOa[u] = done("v", V.tensor_scalar(T.off1[:, 4 * u:4 * u + 4], T.K[:, 4 * u:4 * u + 4], BIG, None, A.mult))
+    need("s", kK[1])
     for e in range(4):
-        kK2 = done("s", Sc.activation(T.K2[quad[e], :], T.K[quad[(e + 1) % 4], :], F.Identity, bias=1024.0 * (-1) ** e))
-    need("v", kOa, kZero, kWin)
-    for u in range(4):
-        if u == 1:
-            need("v", kK2)
-            kOb = done("v", V.tensor_copy(T.off1[:, 8:16], T.K2[:, :]))
-        if u == 2:
-            need("v", kOb)
-        if u:
-            need("v", kSc)
-        kSc = done("v", V.tensor_copy(T.Win[:, :].indirect(T.off1[:, 4 * u:4 * u + 4]), T.zero[:, :]))
-    need("v", kSc)
-    done("v", V.tensor_tensor_scan(T.M[lower, :], T.Win[lower, WA:WA + 512], T.Win[upper, WA:WA + 512], 0.0, A.max, A.mult))
-    kM = done("v", V.tensor_tensor_scan(T.M[upper, :], T.Win[lower, WB:WB + 512], T.Win[upper, WB:WB + 512], 0.0, A.max, A.mult))
-    need("v", kM)
+        kK2 = done("s", Sc.activation(T.K2[quad[e], :], T.K[quad[(e + 1) % 4], :], F.Identity, bias=1024.0 * (-1) ** e, scale=BIG))
+    need("v", kOa[0], kZero, kWin)
     cum = 32
-    kCum = done("v", V.tensor_tensor_scan(T.CW[:, cum:cum + 512], T.M[:, :], T.ones[:, :], 0.0, A.add, A.add))
+
+    def scatter(u):
+        return done("v", V.tensor_copy(T.Win[:, :].indirect(T.off1[:, 4 * u:4 * u + 4]), T.zero[:, :]))
+
+    kSc = scatter(0)
+    kPad = done("v", V.memset(T.XP[:, 512:4 * PL:PL], 0.0))
+    need("v", kSc)
+    kSc = scatter(1)
+    need("v", kK2)
+    kOb = done("v", V.tensor_copy(T.off1[:, 8:16], T.K2[:, :]))
+    kNth = done("v", V.tensor_scalar(T.nthr[:, :], T.n[:, :], -1.0, -0.5, A.mult, A.add))
+    need("v", kOb)
+    kSc = scatter(2)
+    need("v", kPl)
+    done("v", V.transpose(T.CW[:, 0:32], T.Pl[:, :]))
+    need("v", kSc)
+    kSc = scatter(3)
+    kCz = done("v", V.transpose(T.CW[:, cum + 512:cum + 544], T.Pl[:, :]))
+    need("v", kSc)
+    done("v", V.tensor_tensor_scan(T.M[lower, :], T.Win[lower, WA:WA + 512], T.Win[upper, WA:WA + 512], 0.0, A.min, A.mult))
+    kM = done("v", V.tensor_tensor_scan(T.M[upper, :], T.Win[lower, WB:WB + 512], T.Win[upper, WB:WB + 512], 0.0, A.min, A.mult))
+    need("v", kM)
+    kCum = done("v", V.tensor_tensor_scan(T.CW[:, cum:cum + 512], T.M[:, :], T.ones[:, :], 0.0, A.add, A.subtract))
     need("s", kN)
     kThr = done("s", Sc.activation(T.thr[:, :], T.n[:, :], F.Identity, bias=0.5))
+    for half, w in ((lower, WA), (upper, WB)):
+        kGp = done("s", Sc.activation(T.gp[half, :], T.gsh[half, :], F.Identity, bias=cum + UP - w, scale=BIG))
+
+    def plane(t):
+        return T.XP[:, PL * t:PL * t + 512], T.x0[:, t:2048:4]
+
     need("s", ("lx", 16))
     for t in (2, 3):
-        kPlS = done("s", Sc.activation(T.XP[:, PL * t:PL * t + 512], T.x0[:, t:2048:4], F.Copy))
+        done("s", Sc.activation(*plane(t), F.Copy))
     need("s", kCum, kThr)
-    c1 = done("s", Sc.activation(T.J1[:, :], T.CW[:, cum:cum + CS], F.Sign, bias=T.thr[:, 1:2], scale=-1.0, accum_out=T.P1[:, :]))
-    c0 = done("s", Sc.activation(T.J0[:, :], T.CW[:, cum:cum + 512], F.Sign, bias=T.thr[:, 0:1], scale=-1.0, accum_out=T.SRC[:, SE:SE + 1]))
-    need("v", kCum, kThr)
-    kJ2 = done("v", V.tensor_scalar(T.J2[:, :], T.CW[:, cum:cum + 512], T.thr[:, 2:3], 2.0, A.is_lt, A.mult))
-    kJ3 = done("v", V.tensor_scalar(T.J3[:, 1:2 * h3 - 1], T.CW[:, cum + CS:cum + 512], T.thr[:, 1:2], 2.0, A.is_lt, A.mult))
+    c1 = done("s", Sc.activation(T.J1[:, :], T.CW[:, cum:cum + CS], F.Sign, bias=T.thr[:, 1:2], accum_out=T.P1[:, :]))
+    c0 = done("s", Sc.activation(T.J0[:, :], T.CW[:, cum:cum + 512], F.Sign, bias=T.thr[:, 0:1], accum_out=T.SRC[:, SE:SE + 1]))
+    need("v", kCum, kNth)
+    kJ2 = done("v", V.tensor_scalar(T.J2[:, :], T.CW[:, cum:cum + 512], T.nthr[:, 2:3], 2.0, A.is_gt, A.mult))
+    kJ3 = done("v", V.tensor_scalar(T.J3[:, 1:2 * h3 - 1], T.CW[:, cum + CS:cum + 512], T.nthr[:, 1:2], 2.0, A.is_gt, A.mult))
     need("v", kJ2)
     done("v", V.tensor_tensor_scan(T.SRC[:, SE + 2 - 3 * 255:SE + 3:3], T.J2[:, 0:256], T.J2[:, 256:512], -512.0, A.add, A.add))
     need("v", kJ3, c1, kJe)
@@ -202,70 +216,63 @@ def rank_program(g, core, T, topo):
                                           srcs=[T.SRC[:, SE:SE + 4]], dsts=[T.LR[:, 4 * i:4 * i + 4] for i in range(7)])], local_sem=S.out)
     nla = 7 * sent[0]
 
-    kP4 = done("v", V.tensor_scalar(T.p4[:, :], T.pid[:, 0:1], 4, None, A.arith_shift_right))
-    need("v", ("lw", 64))
-    done("v", V.tensor_copy(T.o0[lower, :], T.Lw[lower, :]))
-    kOff0 = done("v", V.tensor_copy(T.o0[upper, :], T.Lw[lower, :]))
-    need("v", kP4)
-    kGp = done("v", V.tensor_scalar(T.gp[:, :], T.p4[:, :], -512.0, float(cum), A.mult, A.add))
-    need("v", kPl)
-    for lo in (0, cum + 512):
-        kCz = done("v", V.transpose(T.CW[:, lo:lo + 32], T.Pl[:, :]))
-    need("v", kOff0, kGp)
+    need("v", ("lw", 128), kGp)
     for u in range(2):
-        kOP = done("v", V.tensor_scalar(T.OP[:, u:64:2], T.o0[:, :], T.gp[:, 0:1], cum + 512.0, A.add, A.min))
+        kOP = done("v", V.tensor_scalar(T.OP[:, u:64:2], T.Lw[:, :], T.gp[:, 0:1], cum + 512.0, A.add, A.min))
     need("v", c0, c2, kPad4)
     kOwn = done("v", V.tensor_copy(T.LR[:, 28:32], T.SRC[:, SE:SE + 4]))
-    need("v", ("lx", 16))
-    for t in (0, 1):
-        done("v", V.tensor_copy(T.XP[:, PL * t:PL * t + 512], T.x0[:, t:2048:4]))
-    kPad = done("v", V.memset(T.XP[:, 512:4 * PL:PL], 0.0))
     need("s", kOP, kCz, kCum)
-    kPs = done("s", Sc.activation(T.Pr[:, 384:1024], T.CW[:, :].indirect(T.OP[:, 24:64]), F.Copy))
+    kPs = done("s", Sc.activation(T.Pr[:, 448:1024], T.CW[:, :].indirect(T.OP[:, 28:64]), F.Copy))
+    kPlS = done("s", Sc.activation(*plane(1), F.Copy))
     need("v", kOP, kCz, kCum)
-    kPv = done("v", V.tensor_copy(T.Pr[:, 0:384], T.CW[:, :].indirect(T.OP[:, 0:24])))
+    kPv = done("v", V.tensor_copy(T.Pr[:, 0:448], T.CW[:, :].indirect(T.OP[:, 0:28])))
+    need("v", ("lx", 16))
+    kPlV = done("v", V.tensor_copy(*plane(0)))
+    need("v", ("lv", 16))
+    kW = done("v", V.quantize_mx(T.QW[:, :], T.SW[:, :], T.wt[:, :]))
+    need("v", kPs, kPv)
+    kPT = done("v", V.transpose(T.PT[:, :], T.Pr[:, :]))
 
     a, b = divmod(r, 2)
     ra = quad[a]
     need("v", ("la", nla), kOwn)
-    kX1 = done("v", V.transpose(T.X1[ra, :], T.LR[ra, :]))
+    for u in range(2):
+        kX1 = done("v", V.transpose(T.X1[ra, u, :], T.LR[ra, :]))
     need("v", kX1)
-    kXd = done("v", V.tensor_copy(T.X1[ra, 16 - 16 * b:32 - 16 * b], T.X1[ra, 16 * b:16 * b + 16]))
-    need("v", kXd)
-    kX3 = done("v", V.transpose(T.X3[ra, :, :], T.X1[ra, :]))
+    for o in quad[:2]:
+        kX3 = done("v", V.transpose(T.X3[o, :, :], T.X1[ra, :, 16 * b:16 * b + 16]))
     need("v", kX3)
-    for o in quad:
-        kO = done("v", V.tensor_scalar(T.O[o, :], T.X3[ra, :, 0:3], 0.5, 256.0, A.mult, A.add))
+    for o in (lower, upper):
+        kO = done("v", V.tensor_scalar(T.O[o, :], T.X3[lower, :, 0:3], 0.5, 256.0, A.mult, A.add))
 
-    def pick(n, t):
-        return T.H[:, 768 * n + t:768 * n + 768:4], T.XP[:, PL * t:PL * t + 513].indirect(T.O[:, 12 * n:12 * n + 12])
+    def pick(lo, hi, t):
+        return T.H[:, 64 * lo + t:64 * hi:4], T.XP[:, PL * t:PL * t + 513].indirect(T.O[:, lo:hi])
 
-    need("s", kO, kPlS, kPad)
+    need("s", kO, kPlS, kPlV, kPad)
     kh = []
-    for n in range(2):
-        for t in (2, 3):
-            k = done("s", Sc.activation(*pick(n, t), F.Copy))
+    for ids, lo, hi, byv, bys in BATCHES:
+        for p in bys:
+            k = done("s", Sc.activation(*pick(*p), F.Copy))
         kh.append(k)
     need("v", kO, kPlS, kPad)
-    eng = {4: [every(0, 4), every(1, 4), every(2, 4), every(3, 4)], 3: [every(0, 4), every(1, 2), every(2, 4)]}
-    flip = {4: [every(1, 4), every(0, 4), every(3, 4), every(2, 4)], 3: [every(1, 4), every(0, 2), every(3, 4)]}
-    for n, batches in enumerate(([(0, 1, 2, 3)], [(4, 5, 6)])):
-        for t in (0, 1):
-            kv = done("v", V.tensor_copy(*pick(n, t)))
+    eng = {4: [every(0, 4), every(1, 4), every(2, 4), every(3, 4)], 3: [every(0, 4), every(1, 2), every(2, 4)], 2: [every(0, 2), every(1, 2)]}
+    flip = {4: [every(1, 4), every(0, 4), every(3, 4), every(2, 4)], 3: [every(1, 4), every(0, 2), every(3, 4)], 2: [every(1, 2), every(0, 2)]}
+    for n, (ids, lo, hi, byv, bys) in enumerate(BATCHES):
+        for p in byv:
+            kv = done("v", V.tensor_copy(*pick(*p)))
         need("v", kv, kh[n])
-        kq = done("v", V.quantize_mx(T.Q[:, 192 * n:192 * n + 192], T.SQ[:, 192 * n:192 * n + 192], T.H[:, 768 * n:768 * n + 768]))
+        q, p = T["Q%d" % n], T["S%d" % n]
+        kq = done("v", V.quantize_mx(q[:, :], p[:, :], T.H[:, 4 * lo:4 * hi]))
         need("g", kq)
         sem = S["a%d" % n]
-        for ids in batches:
-            to = [(peer(r, i), slice(CAP * i, CAP * i + CAP)) for i in ids]
-            fused([(d, T.Q[:, c].bitcast(dt.uint8), T.CR[:, c].bitcast(dt.uint8), sem, m) for (d, c), m in zip(to, eng[len(to)])])
-            fused([(d, T.SQ[:, c], T.SR[:, c], sem, m) for (d, c), m in zip(to, flip[len(to)])])
-    need("v", ("lv", 16))
-    kW = done("v", V.quantize_mx(T.QW[:, :], T.SW[:, :], T.wt[:, :]))
+        to = [(peer(r, i), slice(CAP * i - lo, CAP * i - lo + CAP), slice(CAP * i, CAP * i + CAP)) for i in ids]
+        fused([(d, q[:, c].bitcast(dt.uint8), T.CR[:, e].bitcast(dt.uint8), sem, m) for (d, c, e), m in zip(to, eng[len(to)])])
+        fused([(d, p[:, c], T.SR[:, e], sem, m) for (d, c, e), m in zip(to, flip[len(to)])])
+    need("s", kq)
+    for t in range(4):
+        kHo = done("s", Sc.activation(*pick(20, 24, t), F.Copy))
 
     q0 = quad[0]
-    need("v", kPs, kPv)
-    kPT = done("v", V.transpose(T.PT[:, :], T.Pr[:, :]))
     need("v", kPT)
     kxa = done("v", V.tensor_tensor(T.xa[:, :], T.PT[:, 0:1024:32], T.PT[:, 16:1024:32], A.add))
     need("v", kxa)
@@ -274,31 +281,33 @@ def rank_program(g, core, T, topo):
     kxd = done("v", V.tensor_tensor(T.xd[q0, :], T.xc[q0, :], T.xc[quad[1], :], A.add))
     need("v", kxd)
     for o in quad:
-        kFO = done("v", V.tensor_scalar(T.FO[o, :], T.xd[q0, :], CAP * sum(place.values()) - 1.0, None, A.add))
+        kFO = done("v", V.tensor_scalar(T.FO[o, :], T.xd[q0, :], -1.0, CAP * sum(place.values()) - 1.0, A.mult, A.add))
+    need("v", kHo)
+    kqo = done("v", V.quantize_mx(T.QO[:, :], T.SO[:, :], T.H[:, 1024:1536]))
 
     ts = g.tensor
-    need("t", kW, kq)
-    m0 = done("t", ts.matmul_mx(T.po[:, 0:128], T.QW[:, :], T.SW[:, :], T.Q[:, 256:384], T.SQ[:, 256:384], True, True))
-    need("t", ("a0", 32))
-    m1 = done("t", ts.matmul_mx(T.pa[:, 0:192], T.QW[:, :], T.SW[:, :], T.CR[:, 0:192], T.SR[:, 0:192], True, True))
-    need("t", ("a1", 32))
-    m2 = done("t", ts.matmul_mx(T.pb[:, 0:144], T.QW[:, :], T.SW[:, :], T.CR[:, 192:336], T.SR[:, 192:336], True, True))
+    need("t", kW, kqo)
+    m0 = done("t", ts.matmul_mx(T.po[:, 0:128], T.QW[:, :], T.SW[:, :], T.QO[:, :], T.SO[:, :], True, True))
+    arrived = [("a%d" % n, 32) for n in range(len(BATCHES))]
+    mid = CAP * BATCHES[-1][0][0]
+    need("t", *arrived[:-1])
+    m1 = done("t", ts.matmul_mx(T.pa[:, 0:mid], T.QW[:, :], T.SW[:, :], T.CR[:, 0:mid], T.SR[:, 0:mid], True, True))
+    need("t", arrived[-1])
+    m2 = done("t", ts.matmul_mx(T.pb[:, 0:336 - LAST], T.QW[:, :], T.SW[:, :], T.CR[:, LAST:336], T.SR[:, LAST:336], True, True))
 
     need("s", m0)
     zo = done("s", Sc.activation(T.Z[:, 336:384], T.po[:, 80:128], F.Copy))
     need("s", m1)
-    za = done("s", Sc.activation(T.Z[:, 0:192], T.pa[:, 0:192], F.Copy))
+    za = done("s", Sc.activation(T.Z[:, 0:mid], T.pa[:, 0:mid], F.Copy))
     need("v", m2)
-    zb = done("v", V.tensor_copy(T.Z[:, 192:336], T.pb[:, 0:144]))
+    zb = done("v", V.tensor_copy(T.Z[:, mid:336], T.pb[:, mid - LAST:336 - LAST]))
     need("v", kFO, zo, za, zb)
     need("s", kFO, zo, za, zb)
-    for lo, hi, qn in ((0, 6, "y"), (6, 16, "s")):
-        ky = done("v", V.tensor_copy(T.yv[:, 16 * lo:16 * hi], T.Z[:, 0:384].indirect(T.FO[:, lo:hi])))
-        need("y", ky)
-        g.sync.dma_start(T.y[:, 16 * lo:16 * hi], T.yv[:, 16 * lo:16 * hi]).then_inc(S.ly, 16)
-        ky = done("s", Sc.activation(T.ys[:, 16 * lo:16 * hi], T.Z[:, 0:384].indirect(T.FO[:, 16 + lo:16 + hi]), F.Copy))
-        need(qn, ky)
-        queues[qn].dma_start(T.y[:, 256 + 16 * lo:256 + 16 * hi], T.ys[:, 16 * lo:16 * hi]).then_inc(S.ly, 16)
+    for lo, mid, hi, qn in ((0, 8, 16, "y"), (16, 24, 32, "s")):
+        kv = done("v", V.tensor_copy(T.Y[:, 16 * lo:16 * mid], T.Z[:, 0:384].indirect(T.FO[:, lo:mid])))
+        ks = done("s", Sc.activation(T.Y[:, 16 * mid:16 * hi], T.Z[:, 0:384].indirect(T.FO[:, mid:hi]), F.Copy))
+        need(qn, kv, ks)
+        queues[qn].dma_start(T.y[:, 16 * lo:16 * hi], T.Y[:, 16 * lo:16 * hi]).then_inc(S.ly, 16)
 
     need("g", ("out", sent[0]), ("v", cnt["v"]), ("s", cnt["s"]), ("g", cnt["g"]), ("t", cnt["t"]))
-    need("g", ("ld", 48), ("lw", 64), ("lx", 16), ("lv", 16), ("ly", 64), ("la", nla), ("a0", 32), ("a1", 32))
+    need("g", ("ld", 48), ("lw", 128), ("lx", 16), ("lv", 16), ("ly", 32), ("la", nla), *arrived)

@@ -10,8 +10,8 @@ UP = 1024.0
 WA, WB = 2560, 4608
 CS = 272
 SE = 768
-BATCHES = [((0, 1, 2, 3), 0, 192, [(0, 12, 0), (0, 12, 1)], [(0, 12, 2), (0, 12, 3)]),
-           ((4, 5, 6), 192, 336, [(12, 21, 0), (12, 18, 1)], [(12, 21, 2), (12, 21, 3), (18, 21, 1)])]
+BATCHES = [((0, 1, 2, 3), 0, 192, [(0, 12, 0), (0, 12, 1), (18, 21, 1)], [(0, 12, 2), (0, 12, 3)]),
+           ((4, 5, 6), 192, 336, [(12, 21, 0)], [(12, 21, 2), (12, 21, 3), (12, 18, 1)])]
 LAST = 192
 
 
@@ -24,7 +24,7 @@ SCRATCH = {
     **sb("uint16", EO=8, off1=16, O=24, OP=64, FO=32),
     **sb("float32", Cf=8, X=128, R=128, gsh=1, gp=1, k16=4, n=4, thr=4, nthr=4, K=8, K2=8, P1=1, SRC=SE + 4,
          J0=512, J1=CS, LR=32, Z=384, Y=512, xa=32, xc=32, xd=32),
-    **sb("bfloat16", row=260, E=520, NB=520, MK=260, ones=512, zero=64, Win=6656, M=512, CW=576, Pl=32, J2=512, J3=514 - CS,
+    **sb("bfloat16", row=64, E=520, NB=520, MK=260, ones=512, zero=64, Win=6656, M=512, CW=576, Pl=32, J2=512, J3=514 - CS,
          x0=2048, XP=4 * PL, wt=512, H=1536, Pr=1024, PT=1024),
     **sb("float8_e4m3fn_x4", **{"Q%d" % n: b[2] - b[1] for n, b in enumerate(BATCHES)}, QO=128, QW=128, CR=336),
     **sb("uint8", **{"S%d" % n: b[2] - b[1] for n, b in enumerate(BATCHES)}, SO=128, SW=128, SR=336),
@@ -58,8 +58,9 @@ def rank_program(g, core, T, topo):
     def peer(a, i):
         near = [k for k in range(N) if topo.die(T.cores[k]) == topo.die(T.cores[a])]
         far = [k for k in range(N) if k not in near]
-        j = near.index(a) + i // 2
-        return near[(j + 1) % len(near)] if i % 2 else far[j % len(far)]
+        j = near.index(a)
+        order = [far[(j + k) % len(far)] for k in range(len(far))] + [near[(j + k + 1) % len(near)] for k in range(len(near))]
+        return order[i]
 
     place = {q: i for q in range(N) for i in range(N) if peer(q, i) == r}
 
@@ -70,9 +71,9 @@ def rank_program(g, core, T, topo):
     def iota(ap, n, base=0, cm=0, step=1):
         return done("g", g.iota(ap, [[step, n]], base, cm, allow_small_or_imprecise_dtypes=True))
 
-    g.sync.dma_start(T.D[:, 0:4], T.want[:, :]).then_inc(S.ld, 16)
-    g.scalar.dma_start(T.D[0:112, 4:8], T.want[2:16, :]).then_inc(S.ld, 16)
     g.sync.dma_start(T.D[112:128, 4:8], T.want[0:2, :]).then_inc(S.ld, 16)
+    g.scalar.dma_start(T.D[:, 0:4], T.want[:, :]).then_inc(S.ld, 16)
+    g.sync.dma_start(T.D[0:112, 4:8], T.want[2:16, :]).then_inc(S.ld, 16)
     g.sync.dma_start(T.x0[:, :], T.x[:, :]).then_inc(S.lx, 16)
     g.sync.dma_start(T.wt[:, :], T.w[:, :]).then_inc(S.lv, 16)
     for h in range(8):
@@ -82,7 +83,7 @@ def rank_program(g, core, T, topo):
     kPid = done("g", g.iota(T.pid[:, :], [[0, 4]], 0, 1))
     kK16 = iota(T.k16[:, :], 4, 0, 0, 16)
     kEi = done("g", g.iota(T.Ei[:, :], [[1, 4], [4, 2]], 0, 0))
-    kRow = done("g", g.iota(T.row[:, :], [[-16, 4], [1, 65]], 0, 0, allow_small_or_imprecise_dtypes=True))
+    kRow = iota(T.row[:, :], 64, -1)
     kEe = iota(T.E[:, 64:520:65], 8, 1, step=0)
     kZero = iota(T.zero[:, :], 64, step=0)
     kJe = iota(T.J3[:, 0:2 * h3:2 * h3 - 1], 2, CS - 512, 0, 512 - CS)
@@ -91,42 +92,40 @@ def rank_program(g, core, T, topo):
         lo, hi = place[2 * e], place[2 * e + 1]
         need("g", ("g", cnt["g"]))
         kPl = done("g", g.iota(T.Pl[quad[e], :], [[CAP * (hi - lo), 2], [0, 16]], CAP * lo, 0, allow_small_or_imprecise_dtypes=True))
-    kOnes = done("v", V.memset(T.ones[:, :], 1.0))
+    kWa = done("v", V.memset(T.Win[:, WA:WA + 512], -1.0))
     need("v", kPid)
     kPm = done("v", V.tensor_scalar(T.pm[:, :], T.pid[:, :], 15, None, A.bitwise_and))
     kP43 = done("v", V.tensor_scalar(T.p43[:, :], T.pid[:, 0:1], 4, 3, A.arith_shift_right, A.bitwise_and))
     need("v", kPm, kK16)
     kN = done("v", V.tensor_tensor(T.n[:, :], T.pm[:, :], T.k16[:, :], A.add))
     need("v", kP43, kEi)
-    kGsh = done("v", V.tensor_scalar(T.gsh[:, :], T.p43[:, :], -512.0 / BIG, (WA - UP) / BIG, A.mult, A.add))
     kEO = done("v", V.tensor_copy(T.EO[:, :], T.Ei[:, :]))
-
-    def window(lo):
-        need("s", kOnes)
-        return done("s", Sc.activation(T.Win[:, lo:lo + 512], T.ones[:, :], F.Copy, scale=-1.0))
-
-    window(WA)
+    kGsh = done("v", V.tensor_scalar(T.gsh[:, :], T.p43[:, :], -512.0 / BIG, (WA - UP) / BIG, A.mult, A.add))
+    need("s", kWa)
+    kWin = done("s", Sc.activation(T.Win[:, WB:WB + 512], T.Win[:, WA:WA + 512], F.Copy))
+    need("v", kN, kGsh)
+    done("v", V.tensor_scalar(T.MK[:, 64:260:65], T.n[:, :], 16.0 / BIG, T.gsh[:, 0:1], A.mult, A.add))
+    need("s", kRow, kN, kGsh)
+    for k in range(4):
+        kMK = done("s", Sc.activation(T.MK[:, 65 * k:65 * k + 64], T.row[:, :], F.Relu, bias=T.n[:, k:k + 1], scale=-1.0))
     need("v", ("ld", 48), kEO)
-    kX = done("v", V.tensor_scalar(T.X[:, :], T.D[:, 0:8].indirect(T.EO[:, 0:8]), UP, None, A.add))
-    need("v", kN, kRow)
-    kMK = done("v", V.tensor_scalar(T.MK[:, :], T.row[:, :], T.n[:, 0:1], None, A.is_le))
-    need("v", kX)
-    kR = done("v", V.transpose(T.R[:, :], T.X[:, :]))
-    need("v", kMK, kGsh)
-    kMK = done("v", V.tensor_scalar(T.MK[:, 64:260:65], T.n[:, :], 16.0 / BIG, T.gsh[:, 0:1], A.mult, A.add))
-    need("s", kX, kGsh)
-    kC = done("s", Sc.activation(T.Cf[:, :], T.X[:, 0:128:16], F.Identity, bias=T.gsh[:, 0:1], scale=1.0 / BIG))
-    need("v", kR)
-    need("s", kR)
+    sets = [slice(64 * u, 64 * u + 64) for u in range(2)]
+    kX = [done("v", V.tensor_scalar(T.X[:, sets[u]], T.D[:, 0:8].indirect(T.EO[:, 4 * u:4 * u + 4]), UP, None, A.add)) for u in range(2)]
+    kR = []
+    for u in range(2):
+        need("v", kX[u])
+        kR.append(done("v", V.transpose(T.R[:, sets[u]], T.X[:, sets[u]])))
     kE = {}
     for k in range(8):
-        ops = T.E[:, 65 * k:65 * k + 64], T.R[:, 64 * (k // 4):64 * (k // 4) + 64]
+        ops = T.E[:, 65 * k:65 * k + 64], T.R[:, sets[k // 4]]
         own = T.X[:, 16 * k:16 * k + 1]
-        if k >= 5:
+        qn = "s" if k % 4 >= 2 else "v"
+        need(qn, kR[k // 4])
+        if qn == "s":
             kE[k] = done("s", Sc.activation(*ops, F.Abs, bias=own, scale=-1.0))
         else:
             kE[k] = done("v", V.tensor_scalar(*ops, own, None, A.not_equal))
-    kWin = window(WB)
+    kC = done("s", Sc.activation(T.Cf[:, :], T.X[:, 0:128:16], F.Identity, bias=T.gsh[:, 0:1], scale=1.0 / BIG))
     kNB, kK, kOa, kOb, kK2 = {}, {}, {}, {}, {}
     for u in range(2):
         need("v", kMK, kEe, *[kE[k] for k in range(4 * u, 4 * u + 4)])
@@ -140,6 +139,7 @@ def rank_program(g, core, T, topo):
     need("s", kK[1])
     for e in range(4):
         kK2 = done("s", Sc.activation(T.K2[quad[e], :], T.K[quad[(e + 1) % 4], :], F.Identity, bias=1024.0 * (-1) ** e, scale=BIG))
+    kOnes = done("s", Sc.activation(T.ones[:, :], T.E[:, 0:512], F.Identity, bias=1.0, scale=0.0))
     need("v", kOa[0], kZero, kWin)
     cum = 32
 
@@ -163,7 +163,7 @@ def rank_program(g, core, T, topo):
     need("v", kSc)
     done("v", V.tensor_tensor_scan(T.M[lower, :], T.Win[lower, WA:WA + 512], T.Win[upper, WA:WA + 512], 0.0, A.min, A.mult))
     kM = done("v", V.tensor_tensor_scan(T.M[upper, :], T.Win[lower, WB:WB + 512], T.Win[upper, WB:WB + 512], 0.0, A.min, A.mult))
-    need("v", kM)
+    need("v", kM, kOnes)
     kCum = done("v", V.tensor_tensor_scan(T.CW[:, cum:cum + 512], T.M[:, :], T.ones[:, :], 0.0, A.add, A.subtract))
     need("s", kN)
     kThr = done("s", Sc.activation(T.thr[:, :], T.n[:, :], F.Identity, bias=0.5))
@@ -174,8 +174,7 @@ def rank_program(g, core, T, topo):
         return T.XP[:, PL * t:PL * t + 512], T.x0[:, t:2048:4]
 
     need("s", ("lx", 16))
-    for t in (2, 3):
-        done("s", Sc.activation(*plane(t), F.Copy))
+    done("s", Sc.activation(*plane(3), F.Copy))
     need("s", kCum, kThr)
     c1 = done("s", Sc.activation(T.J1[:, :], T.CW[:, cum:cum + CS], F.Sign, bias=T.thr[:, 1:2], accum_out=T.P1[:, :]))
     c0 = done("s", Sc.activation(T.J0[:, :], T.CW[:, cum:cum + 512], F.Sign, bias=T.thr[:, 0:1], accum_out=T.SRC[:, SE:SE + 1]))
@@ -223,7 +222,8 @@ def rank_program(g, core, T, topo):
     kOwn = done("v", V.tensor_copy(T.LR[:, 28:32], T.SRC[:, SE:SE + 4]))
     need("s", kOP, kCz, kCum)
     kPs = done("s", Sc.activation(T.Pr[:, 448:1024], T.CW[:, :].indirect(T.OP[:, 28:64]), F.Copy))
-    kPlS = done("s", Sc.activation(*plane(1), F.Copy))
+    for t in (2, 1):
+        kPlS = done("s", Sc.activation(*plane(t), F.Copy))
     need("v", kOP, kCz, kCum)
     kPv = done("v", V.tensor_copy(T.Pr[:, 0:448], T.CW[:, :].indirect(T.OP[:, 0:28])))
     need("v", ("lx", 16))
@@ -258,9 +258,8 @@ def rank_program(g, core, T, topo):
     eng = {4: [every(0, 4), every(1, 4), every(2, 4), every(3, 4)], 3: [every(0, 4), every(1, 2), every(2, 4)], 2: [every(0, 2), every(1, 2)]}
     flip = {4: [every(1, 4), every(0, 4), every(3, 4), every(2, 4)], 3: [every(1, 4), every(0, 2), every(3, 4)], 2: [every(1, 2), every(0, 2)]}
     for n, (ids, lo, hi, byv, bys) in enumerate(BATCHES):
-        for p in byv:
-            kv = done("v", V.tensor_copy(*pick(*p)))
-        need("v", kv, kh[n])
+        kv = [done("v", V.tensor_copy(*pick(*p))) for p in byv]
+        need("v", kh[n], *[k for k, p in zip(kv, byv) if 16 * p[0] < hi])
         q, p = T["Q%d" % n], T["S%d" % n]
         kq = done("v", V.quantize_mx(q[:, :], p[:, :], T.H[:, 4 * lo:4 * hi]))
         need("g", kq)
@@ -303,7 +302,7 @@ def rank_program(g, core, T, topo):
     zb = done("v", V.tensor_copy(T.Z[:, mid:336], T.pb[:, mid - LAST:336 - LAST]))
     need("v", kFO, zo, za, zb)
     need("s", kFO, zo, za, zb)
-    for lo, mid, hi, qn in ((0, 8, 16, "y"), (16, 24, 32, "s")):
+    for lo, mid, hi, qn in ((0, 8, 14, "y"), (14, 24, 32, "s")):
         kv = done("v", V.tensor_copy(T.Y[:, 16 * lo:16 * mid], T.Z[:, 0:384].indirect(T.FO[:, lo:mid])))
         ks = done("s", Sc.activation(T.Y[:, 16 * mid:16 * hi], T.Z[:, 0:384].indirect(T.FO[:, mid:hi]), F.Copy))
         need(qn, kv, ks)

from concourse.bass import DstId, RemoteDMATransfer
from concourse.mybir import dt, AluOpType, ActivationFunctionType

A = AluOpType
F = ActivationFunctionType
CAP = 48
PL = 528
BIG = 8192.0
UP = 1024.0
WA, WB = 2560, 4608
CS = 272
SE = 768
BATCHES = [((0, 1, 2, 3), 0, 192, [(0, 12, 0), (0, 12, 1), (18, 21, 1)], [(0, 12, 2), (0, 12, 3)]),
           ((4, 5, 6), 192, 336, [(12, 21, 0)], [(12, 21, 2), (12, 21, 3), (12, 18, 1)])]
LAST = 192


def sb(kind, **widths):
    return {k: ("sbuf", [128, n], kind) for k, n in widths.items()}


SCRATCH = {
    **sb("int32", Lw=32, D=8, Ei=8, pid=4, pm=4, p43=1),
    **sb("uint16", EO=8, off1=16, O=24, OP=64, FO=32),
    **sb("float32", Cf=8, X=128, R=128, gsh=1, gp=1, k16=4, n=4, thr=4, nthr=4, K=8, K2=8, P1=1, SRC=SE + 4,
         J0=512, J1=CS, LR=32, Z=384, Y=512, xa=32, xc=32, xd=32),
    **sb("bfloat16", row=64, E=520, NB=520, MK=260, ones=512, zero=64, Win=6656, M=512, CW=576, Pl=32, J2=512, J3=514 - CS,
         x0=2048, XP=4 * PL, wt=512, H=1536, Pr=1024, PT=1024),
    **sb("float8_e4m3fn_x4", **{"Q%d" % n: b[2] - b[1] for n, b in enumerate(BATCHES)}, QO=128, QW=128, CR=336),
    **sb("uint8", **{"S%d" % n: b[2] - b[1] for n, b in enumerate(BATCHES)}, SO=128, SW=128, SR=336),
    "X1": ("sbuf", [128, 2, 32], "float32"), "X3": ("sbuf", [128, 8, 4], "float32"),
    "pa": ("psum", [128, 512], "float32"), "pb": ("psum", [128, 512], "float32"), "po": ("psum", [128, 512], "float32"),
}
SEMAPHORES = ["v", "s", "g", "t", "ld", "lw", "lx", "lv", "ly", "la", "out"] + ["a%d" % n for n in range(len(BATCHES))]


def rank_program(g, core, T, topo):
    r = T.rank_of(core)
    if r is None:
        return
    N = len(T.cores)
    S = T.sem
    cnt = {"v": 0, "s": 0, "g": 0, "t": 0}
    queues = {"v": g.vector, "s": g.scalar, "g": g, "t": g.tensor, "y": g.sync}
    waited = {}

    def need(qn, *toks):
        for name, n in toks:
            if waited.get((qn, name), 0) < n:
                waited[(qn, name)] = n
                queues[qn].wait_ge(S[name], n)

    def done(qn, ins):
        ins.then_inc(S[qn], 1)
        cnt[qn] += 1
        return (qn, cnt[qn])

    def peer(a, i):
        near = [k for k in range(N) if topo.die(T.cores[k]) == topo.die(T.cores[a])]
        far = [k for k in range(N) if k not in near]
        j = near.index(a)
        order = [far[(j + k) % len(far)] for k in range(len(far))] + [near[(j + k + 1) % len(near)] for k in range(len(near))]
        return order[i]

    place = {q: i for q in range(N) for i in range(N) if peer(q, i) == r}

    V, Sc = g.vector, g.scalar
    lower, upper = slice(0, 64), slice(64, 128)
    quad = [slice(32 * e, 32 * e + 32) for e in range(4)]

    def iota(ap, n, base=0, cm=0, step=1):
        return done("g", g.iota(ap, [[step, n]], base, cm, allow_small_or_imprecise_dtypes=True))

    g.sync.dma_start(T.D[112:128, 4:8], T.want[0:2, :]).then_inc(S.ld, 16)
    g.scalar.dma_start(T.D[:, 0:4], T.want[:, :]).then_inc(S.ld, 16)
    g.sync.dma_start(T.D[0:112, 4:8], T.want[2:16, :]).then_inc(S.ld, 16)
    g.sync.dma_start(T.x0[:, :], T.x[:, :]).then_inc(S.lx, 16)
    g.sync.dma_start(T.wt[:, :], T.w[:, :]).then_inc(S.lv, 16)
    for h in range(8):
        g.sync.dma_start(T.Lw[16 * h:16 * h + 16, :], T.want[:, :]).then_inc(S.lw, 16)

    h3 = (512 - CS) // 2 + 1
    kPid = done("g", g.iota(T.pid[:, :], [[0, 4]], 0, 1))
    kK16 = iota(T.k16[:, :], 4, 0, 0, 16)
    kEi = done("g", g.iota(T.Ei[:, :], [[1, 4], [4, 2]], 0, 0))
    kRow = iota(T.row[:, :], 64, -1)
    kEe = iota(T.E[:, 64:520:65], 8, 1, step=0)
    kZero = iota(T.zero[:, :], 64, step=0)
    kJe = iota(T.J3[:, 0:2 * h3:2 * h3 - 1], 2, CS - 512, 0, 512 - CS)
    kPad4 = iota(T.SRC[:, SE + 3:SE + 4], 1, step=0)
    for e in range(4):
        lo, hi = place[2 * e], place[2 * e + 1]
        need("g", ("g", cnt["g"]))
        kPl = done("g", g.iota(T.Pl[quad[e], :], [[CAP * (hi - lo), 2], [0, 16]], CAP * lo, 0, allow_small_or_imprecise_dtypes=True))
    kWa = done("v", V.memset(T.Win[:, WA:WA + 512], -1.0))
    need("v", kPid)
    kPm = done("v", V.tensor_scalar(T.pm[:, :], T.pid[:, :], 15, None, A.bitwise_and))
    kP43 = done("v", V.tensor_scalar(T.p43[:, :], T.pid[:, 0:1], 4, 3, A.arith_shift_right, A.bitwise_and))
    need("v", kPm, kK16)
    kN = done("v", V.tensor_tensor(T.n[:, :], T.pm[:, :], T.k16[:, :], A.add))
    need("v", kP43, kEi)
    kEO = done("v", V.tensor_copy(T.EO[:, :], T.Ei[:, :]))
    kGsh = done("v", V.tensor_scalar(T.gsh[:, :], T.p43[:, :], -512.0 / BIG, (WA - UP) / BIG, A.mult, A.add))
    need("s", kWa)
    kWin = done("s", Sc.activation(T.Win[:, WB:WB + 512], T.Win[:, WA:WA + 512], F.Copy))
    need("v", kN, kGsh)
    done("v", V.tensor_scalar(T.MK[:, 64:260:65], T.n[:, :], 16.0 / BIG, T.gsh[:, 0:1], A.mult, A.add))
    need("s", kRow, kN, kGsh)
    for k in range(4):
        kMK = done("s", Sc.activation(T.MK[:, 65 * k:65 * k + 64], T.row[:, :], F.Relu, bias=T.n[:, k:k + 1], scale=-1.0))
    need("v", ("ld", 48), kEO)
    sets = [slice(64 * u, 64 * u + 64) for u in range(2)]
    kX = [done("v", V.tensor_scalar(T.X[:, sets[u]], T.D[:, 0:8].indirect(T.EO[:, 4 * u:4 * u + 4]), UP, None, A.add)) for u in range(2)]
    kR = []
    for u in range(2):
        need("v", kX[u])
        kR.append(done("v", V.transpose(T.R[:, sets[u]], T.X[:, sets[u]])))
    kE = {}
    for k in range(8):
        ops = T.E[:, 65 * k:65 * k + 64], T.R[:, sets[k // 4]]
        own = T.X[:, 16 * k:16 * k + 1]
        qn = "s" if k % 4 >= 2 else "v"
        need(qn, kR[k // 4])
        if qn == "s":
            kE[k] = done("s", Sc.activation(*ops, F.Abs, bias=own, scale=-1.0))
        else:
            kE[k] = done("v", V.tensor_scalar(*ops, own, None, A.not_equal))
    kC = done("s", Sc.activation(T.Cf[:, :], T.X[:, 0:128:16], F.Identity, bias=T.gsh[:, 0:1], scale=1.0 / BIG))
    kNB, kK, kOa, kOb, kK2 = {}, {}, {}, {}, {}
    for u in range(2):
        need("v", kMK, kEe, *[kE[k] for k in range(4 * u, 4 * u + 4)])
        kNB[u] = done("v", V.tensor_tensor_scan(T.NB[:, 260 * u:260 * u + 260], T.E[:, 260 * u:260 * u + 260], T.MK[:, :], 1.0, A.min, A.add))
    for u in range(2):
        need("v", kNB[u], kC)
        kK[u] = done("v", V.tensor_tensor(T.K[:, 4 * u:4 * u + 4], T.NB[:, 260 * u + 64:260 * u + 260:65], T.Cf[:, 4 * u:4 * u + 4], A.min))
    for u in range(2):
        need("v", kK[u])
        kOa[u] = done("v", V.tensor_scalar(T.off1[:, 4 * u:4 * u + 4], T.K[:, 4 * u:4 * u + 4], BIG, None, A.mult))
    need("s", kK[1])
    for e in range(4):
        kK2 = done("s", Sc.activation(T.K2[quad[e], :], T.K[quad[(e + 1) % 4], :], F.Identity, bias=1024.0 * (-1) ** e, scale=BIG))
    kOnes = done("s", Sc.activation(T.ones[:, :], T.E[:, 0:512], F.Identity, bias=1.0, scale=0.0))
    need("v", kOa[0], kZero, kWin)
    cum = 32

    def scatter(u):
        return done("v", V.tensor_copy(T.Win[:, :].indirect(T.off1[:, 4 * u:4 * u + 4]), T.zero[:, :]))

    kSc = scatter(0)
    kPad = done("v", V.memset(T.XP[:, 512:4 * PL:PL], 0.0))
    need("v", kSc)
    kSc = scatter(1)
    need("v", kK2)
    kOb = done("v", V.tensor_copy(T.off1[:, 8:16], T.K2[:, :]))
    kNth = done("v", V.tensor_scalar(T.nthr[:, :], T.n[:, :], -1.0, -0.5, A.mult, A.add))
    need("v", kOb)
    kSc = scatter(2)
    need("v", kPl)
    done("v", V.transpose(T.CW[:, 0:32], T.Pl[:, :]))
    need("v", kSc)
    kSc = scatter(3)
    kCz = done("v", V.transpose(T.CW[:, cum + 512:cum + 544], T.Pl[:, :]))
    need("v", kSc)
    done("v", V.tensor_tensor_scan(T.M[lower, :], T.Win[lower, WA:WA + 512], T.Win[upper, WA:WA + 512], 0.0, A.min, A.mult))
    kM = done("v", V.tensor_tensor_scan(T.M[upper, :], T.Win[lower, WB:WB + 512], T.Win[upper, WB:WB + 512], 0.0, A.min, A.mult))
    need("v", kM, kOnes)
    kCum = done("v", V.tensor_tensor_scan(T.CW[:, cum:cum + 512], T.M[:, :], T.ones[:, :], 0.0, A.add, A.subtract))
    need("s", kN)
    kThr = done("s", Sc.activation(T.thr[:, :], T.n[:, :], F.Identity, bias=0.5))
    for half, w in ((lower, WA), (upper, WB)):
        kGp = done("s", Sc.activation(T.gp[half, :], T.gsh[half, :], F.Identity, bias=cum + UP - w, scale=BIG))

    def plane(t):
        return T.XP[:, PL * t:PL * t + 512], T.x0[:, t:2048:4]

    need("s", ("lx", 16))
    done("s", Sc.activation(*plane(3), F.Copy))
    need("s", kCum, kThr)
    c1 = done("s", Sc.activation(T.J1[:, :], T.CW[:, cum:cum + CS], F.Sign, bias=T.thr[:, 1:2], accum_out=T.P1[:, :]))
    c0 = done("s", Sc.activation(T.J0[:, :], T.CW[:, cum:cum + 512], F.Sign, bias=T.thr[:, 0:1], accum_out=T.SRC[:, SE:SE + 1]))
    need("v", kCum, kNth)
    kJ2 = done("v", V.tensor_scalar(T.J2[:, :], T.CW[:, cum:cum + 512], T.nthr[:, 2:3], 2.0, A.is_gt, A.mult))
    kJ3 = done("v", V.tensor_scalar(T.J3[:, 1:2 * h3 - 1], T.CW[:, cum + CS:cum + 512], T.nthr[:, 1:2], 2.0, A.is_gt, A.mult))
    need("v", kJ2)
    done("v", V.tensor_tensor_scan(T.SRC[:, SE + 2 - 3 * 255:SE + 3:3], T.J2[:, 0:256], T.J2[:, 256:512], -512.0, A.add, A.add))
    need("v", kJ3, c1, kJe)
    c2 = done("v", V.tensor_tensor_scan(T.SRC[:, SE + 1 - 3 * (h3 - 1):SE + 2:3], T.J3[:, 0:h3], T.J3[:, h3:2 * h3], T.P1[:, 0:1], A.add, A.add))
    sent = [0]

    def mask(dst, pick):
        es = topo.engines(core, dst)
        m = 0
        for j in pick(len(es)):
            m |= 1 << es[j]
            sent[0] += 1
        return m

    def at(dst):
        rid, pid, _ = topo.addr(dst)
        return DstId(rid=rid, pnc=pid)

    def fused(items):
        tr = []
        for d, src, out, sem, pick in items:
            c = T.cores[d]
            tr.append(RemoteDMATransfer(dst_ids=[at(c)], dma_engine_mask=mask(c, pick), remote_sem=sem, src=src, dst=out))
        g.remote_dma_fused(tr, local_sem=S.out)

    def every(i, n):
        return lambda ne: range(i, ne, n)

    need("g", c0, c2, kPad4)
    to = [T.cores[q] for q in sorted(place, key=place.get)[:7]]
    g.remote_dma_fused([RemoteDMATransfer(dst_ids=[at(c) for c in to], dma_engine_mask=mask(to[0], every(0, 1)), remote_sem=S.la,
                                          srcs=[T.SRC[:, SE:SE + 4]], dsts=[T.LR[:, 4 * i:4 * i + 4] for i in range(7)])], local_sem=S.out)
    nla = 7 * sent[0]

    need("v", ("lw", 128), kGp)
    for u in range(2):
        kOP = done("v", V.tensor_scalar(T.OP[:, u:64:2], T.Lw[:, :], T.gp[:, 0:1], cum + 512.0, A.add, A.min))
    need("v", c0, c2, kPad4)
    kOwn = done("v", V.tensor_copy(T.LR[:, 28:32], T.SRC[:, SE:SE + 4]))
    need("s", kOP, kCz, kCum)
    kPs = done("s", Sc.activation(T.Pr[:, 448:1024], T.CW[:, :].indirect(T.OP[:, 28:64]), F.Copy))
    for t in (2, 1):
        kPlS = done("s", Sc.activation(*plane(t), F.Copy))
    need("v", kOP, kCz, kCum)
    kPv = done("v", V.tensor_copy(T.Pr[:, 0:448], T.CW[:, :].indirect(T.OP[:, 0:28])))
    need("v", ("lx", 16))
    kPlV = done("v", V.tensor_copy(*plane(0)))
    need("v", ("lv", 16))
    kW = done("v", V.quantize_mx(T.QW[:, :], T.SW[:, :], T.wt[:, :]))
    need("v", kPs, kPv)
    kPT = done("v", V.transpose(T.PT[:, :], T.Pr[:, :]))

    a, b = divmod(r, 2)
    ra = quad[a]
    need("v", ("la", nla), kOwn)
    for u in range(2):
        kX1 = done("v", V.transpose(T.X1[ra, u, :], T.LR[ra, :]))
    need("v", kX1)
    for o in quad[:2]:
        kX3 = done("v", V.transpose(T.X3[o, :, :], T.X1[ra, :, 16 * b:16 * b + 16]))
    need("v", kX3)
    for o in (lower, upper):
        kO = done("v", V.tensor_scalar(T.O[o, :], T.X3[lower, :, 0:3], 0.5, 256.0, A.mult, A.add))

    def pick(lo, hi, t):
        return T.H[:, 64 * lo + t:64 * hi:4], T.XP[:, PL * t:PL * t + 513].indirect(T.O[:, lo:hi])

    need("s", kO, kPlS, kPlV, kPad)
    kh = []
    for ids, lo, hi, byv, bys in BATCHES:
        for p in bys:
            k = done("s", Sc.activation(*pick(*p), F.Copy))
        kh.append(k)
    need("v", kO, kPlS, kPad)
    eng = {4: [every(0, 4), every(1, 4), every(2, 4), every(3, 4)], 3: [every(0, 4), every(1, 2), every(2, 4)], 2: [every(0, 2), every(1, 2)]}
    flip = {4: [every(1, 4), every(0, 4), every(3, 4), every(2, 4)], 3: [every(1, 4), every(0, 2), every(3, 4)], 2: [every(1, 2), every(0, 2)]}
    for n, (ids, lo, hi, byv, bys) in enumerate(BATCHES):
        kv = [done("v", V.tensor_copy(*pick(*p))) for p in byv]
        need("v", kh[n], *[k for k, p in zip(kv, byv) if 16 * p[0] < hi])
        q, p = T["Q%d" % n], T["S%d" % n]
        kq = done("v", V.quantize_mx(q[:, :], p[:, :], T.H[:, 4 * lo:4 * hi]))
        need("g", kq)
        sem = S["a%d" % n]
        to = [(peer(r, i), slice(CAP * i - lo, CAP * i - lo + CAP), slice(CAP * i, CAP * i + CAP)) for i in ids]
        fused([(d, q[:, c].bitcast(dt.uint8), T.CR[:, e].bitcast(dt.uint8), sem, m) for (d, c, e), m in zip(to, eng[len(to)])])
        fused([(d, p[:, c], T.SR[:, e], sem, m) for (d, c, e), m in zip(to, flip[len(to)])])
    need("s", kq)
    for t in range(4):
        kHo = done("s", Sc.activation(*pick(20, 24, t), F.Copy))

    q0 = quad[0]
    need("v", kPT)
    kxa = done("v", V.tensor_tensor(T.xa[:, :], T.PT[:, 0:1024:32], T.PT[:, 16:1024:32], A.add))
    need("v", kxa)
    kxc = done("v", V.tensor_tensor(T.xc[lower, :], T.xa[lower, :], T.xa[upper, :], A.add))
    need("v", kxc)
    kxd = done("v", V.tensor_tensor(T.xd[q0, :], T.xc[q0, :], T.xc[quad[1], :], A.add))
    need("v", kxd)
    for o in quad:
        kFO = done("v", V.tensor_scalar(T.FO[o, :], T.xd[q0, :], -1.0, CAP * sum(place.values()) - 1.0, A.mult, A.add))
    need("v", kHo)
    kqo = done("v", V.quantize_mx(T.QO[:, :], T.SO[:, :], T.H[:, 1024:1536]))

    ts = g.tensor
    need("t", kW, kqo)
    m0 = done("t", ts.matmul_mx(T.po[:, 0:128], T.QW[:, :], T.SW[:, :], T.QO[:, :], T.SO[:, :], True, True))
    arrived = [("a%d" % n, 32) for n in range(len(BATCHES))]
    mid = CAP * BATCHES[-1][0][0]
    need("t", *arrived[:-1])
    m1 = done("t", ts.matmul_mx(T.pa[:, 0:mid], T.QW[:, :], T.SW[:, :], T.CR[:, 0:mid], T.SR[:, 0:mid], True, True))
    need("t", arrived[-1])
    m2 = done("t", ts.matmul_mx(T.pb[:, 0:336 - LAST], T.QW[:, :], T.SW[:, :], T.CR[:, LAST:336], T.SR[:, LAST:336], True, True))

    need("s", m0)
    zo = done("s", Sc.activation(T.Z[:, 336:384], T.po[:, 80:128], F.Copy))
    need("s", m1)
    za = done("s", Sc.activation(T.Z[:, 0:mid], T.pa[:, 0:mid], F.Copy))
    need("v", m2)
    zb = done("v", V.tensor_copy(T.Z[:, mid:336], T.pb[:, mid - LAST:336 - LAST]))
    need("v", kFO, zo, za, zb)
    need("s", kFO, zo, za, zb)
    for lo, mid, hi, qn in ((0, 8, 14, "y"), (14, 24, 32, "s")):
        kv = done("v", V.tensor_copy(T.Y[:, 16 * lo:16 * mid], T.Z[:, 0:384].indirect(T.FO[:, lo:mid])))
        ks = done("s", Sc.activation(T.Y[:, 16 * mid:16 * hi], T.Z[:, 0:384].indirect(T.FO[:, mid:hi]), F.Copy))
        need(qn, kv, ks)
        queues[qn].dma_start(T.y[:, 16 * lo:16 * hi], T.Y[:, 16 * lo:16 * hi]).then_inc(S.ly, 16)

    need("g", ("out", sent[0]), ("v", cnt["v"]), ("s", cnt["s"]), ("g", cnt["g"]), ("t", cnt["t"]))
    need("g", ("ld", 48), ("lw", 128), ("lx", 16), ("lv", 16), ("ly", 32), ("la", nla), *arrived)
